import numpy as np, ml_dtypes
CORES = [10,34,74,98]
N = 4
BF = ml_dtypes.bfloat16
def gentries(a):
    return np.ascontiguousarray(a.reshape(8, 16, -1).transpose(0, 2, 1)).reshape(8, -1)
def gtable(e):
    e = np.asarray(e); return np.ascontiguousarray(e.reshape(8, -1, 16).transpose(0, 2, 1)).reshape(128, -1).astype(np.int32)
def f(rng, *shape):
    return (rng.standard_normal(shape, dtype=np.float32) * np.exp2(rng.integers(-2, 3, shape[:-1] + (1,)))).astype(BF)
def wide(rng, *shape):
    v = f(rng, *shape).astype(np.float32); k = shape[:-2] + (1, shape[-1])
    return (v * np.exp2(rng.integers(-6, 7, k)) * (rng.random(k) > 0.0625)).astype(BF)
W, K, S, RO, FI, CAP = 4096, 2048, 3, 3, 6, 128
def parts(rng):
    b = rng.random((N, 8, S, W)) < rng.choice(np.array([0.5, 0.6, 0.75]), (N, 8, S, 1)); b[..., 0] = True; b[..., W - 1] = True
    nx = np.zeros((N, 8, S, W), np.int64); cur = np.zeros((N, 8, S, K), np.int64)
    for a in range(N):
        for g in range(8):
            for i in range(S):
                v = np.nonzero(b[a, g, i])[0]
                nx[a, g, i] = rng.choice(v, W); nx[a, g, i, v] = rng.permutation(v); cur[a, g, i] = rng.choice(v, K)
    return b, nx, cur, rng.integers(0, S, (N, 8, K)), rng.integers(0, W, (N, 8, W))
def pack(x, b, nx, cur, typ, fro, w):
    mem = np.add.reduce(b.astype(np.int64) << np.arange(S)[:, None], axis=2)
    return {"x": x.astype(BF).reshape(N, 128, W), "nxt": nx.reshape(N, 8, S * W).astype(np.int32), "mem": mem.astype(np.int32), "fro": fro.astype(np.int32),
            "cur": np.stack([gtable(a.reshape(8, S * K)) for a in cur]), "typ": np.stack([gtable(a) for a in typ]), "w0": w.astype(BF).reshape(N, 128, K)}
def setup_inputs(rng):
    b, nx, cur, typ, fro = parts(rng)
    return pack(f(rng, N, 128, W), b, nx, cur, typ, fro, f(rng, N, 128, K))
def setup_inputs_room(rng):
    b, nx, cur, typ, fro = parts(rng)
    x = np.minimum(f(rng, N, 128, W).astype(np.float32), 24); w = f(rng, N, 128, K).astype(np.float32).reshape(N, 8, 16, K)
    w[:, ::2] = np.abs(w[:, ::2]) + 32; w[:, 1] = np.abs(w[:, 1]) + 32
    at = np.take_along_axis(cur, typ[:, :, None, :], 2)[:, :, 0]
    for q in range(FI): at = np.take_along_axis(nx.reshape(N, 8, S * W), typ * W + at, 2)
    z = np.where(typ == S - 1, 0, typ + 1)
    for a in range(N):
        m, zz, cc, i = at[a, 1], z[a, 1], cur[a, 1], a % S
        o = rng.permutation(np.arange(1, K - 1)); o = o[b[a, 1, zz[o], m[o]] & (m[o] > 0) & (m[o] < W - 2)]
        o = rng.permutation(o[np.unique(m[o], return_index=True)[1]])
        by = [o[zz[o] == j] for j in range(S)]
        cc[zz, np.arange(K)] = m
        for j in range(S): cc[j, by[j][:3]] = (0, W - 2, W - 1)
        u, v, p, q, e1, e2 = by[i][3:9]
        ends = [K - 1, 0] if a % 2 == 0 else [0, K - 1]
        typ[a, 1, ends] = typ[a, 1, [u, v]]; cc[:, ends] = cc[:, [u, v]]
        cc[i, ends[0]] = m[q]; cc[i, p] = m[v]
        r = rng.choice(np.nonzero(~b[a, 1, i, :W - 2])[0]); nx[a, 1, i, r] = nx[a, 1, i, m[e1]]; cc[i, e1] = r; cc[i, e2] = r
        b[a, 1, typ[a, 1, [u, p]], m[[u, p]]] = False
    for a in range(N):
        for g in range(0, 8, 2):
            m = at[a, g]; zz = z[a, g]; e = rng.permutation(np.nonzero(b[a, g, zz, m])[0])
            k = int(rng.choice(np.array([0, 1, CAP - 1, CAP, CAP + 1, len(e)])))
            if a < 2: k = ((CAP, CAP + 1, CAP - 1, 0), (1, CAP, len(e), CAP + 1))[a][g // 2]
            cur[a, g, zz[e], e] = m[e]
            one = e[(zz[e] == 0) & (m[e] != 0)][:1] if k == 1 else e[:0]
            e = np.concatenate([one, e])[:k]; k = len(e)
            c = rng.choice(np.concatenate([rng.permutation(W)[:int(rng.choice(np.array([24, 150, 600, W])))], m[e[:k // 4]]]), k)
            cur[a, g, zz[e], e] = np.where(c == m[e], (c + 1) % W, c)
            cur[a, g, 0, one] = 0
    return pack(x, b, nx, cur, typ, fro, w)
def setup_inputs_ties(rng):
    b, nx, cur, typ, fro = parts(rng)
    x = 4.0 * rng.integers(-3, 4, (N, 8, 16, W)); w = 4.0 * rng.integers(-3, 4, (N, 8, 16, K))
    x[::2, 5] = rng.choice(np.array([7.96875, 8, 8, 8, 8.0625]), (N // 2, 16, W)); x[1::2, 5] = 64
    w[:, 5] = rng.choice(np.array([-1.0, 1.0]), (N, 16, K)) * np.exp2(-1.0 * rng.integers(14, 21, (N, 16, K)))
    return pack(x, b, nx, cur, typ, fro, w)
def setup_inputs_alike(rng):
    b, nx, cur, typ, fro = parts(rng)
    cur[:, 0] = rng.choice(np.array([0, W - 1]), (N, S, K)); nx[:, 1] = rng.choice(np.array([0, 3, W // 2, W - 1]), (N, S, W)); nx[:, 2] = np.arange(W)
    fro[:, 3] = rng.choice(np.array([0, W - 1]), (N, W)); b[:, 4] = True; b[:, 5] = False; typ[:, 6] = 0; cur[:, 7] = np.repeat(cur[:, 7, :1], S, axis=1)
    return pack(f(rng, N, 128, W), b, nx, cur, typ, fro, f(rng, N, 128, K))
def setup_inputs_hot(rng):
    b, nx, cur, typ, fro = parts(rng)
    sh = rng.choice(np.array([-64, 0, 64]), (N, 8, 1, 1)); sh[0, :4, 0, 0] = (-64, 64, -64, 0); sh[1, 4:, 0, 0] = (0, -64, 64, -64)
    b[rng.random((N, 8)) < 0.3] = True; b[0, 0] = True; b[1, 5] = True
    x = f(rng, N, 128, W).reshape(N, 8, 16, W); w = f(rng, N, 128, K).astype(np.float32).reshape(N, 8, 16, K) + sh
    for g in (3, 6):
        b[:, g] = True; w[:, g] = 4
        x[::2, g] = (rng.integers(0, 25, x[::2, g].shape) * 0.125).astype(BF); x[1::2, g] = (rng.integers(-32, -7, x[1::2, g].shape) * 0.125).astype(BF)
    for a in range(0, N, 2):
        o = np.concatenate([CAP // 2 + rng.permutation(CAP // 2)[:CAP // 4], CAP + rng.permutation(K - CAP)[:CAP // 8]])
        w[a, 6][:, o] = 1000
    return pack(x, b, nx, cur, typ, fro, w)
def setup_inputs_spread(rng):
    b, nx, cur, typ, fro = parts(rng)
    return pack(wide(rng, N, 128, W), b, nx, cur, typ, fro, wide(rng, N, 128, K))
def check_inputs(d):
    bad = []
    for k, hi in (("nxt", W - 1), ("mem", 2 ** S - 1), ("fro", W - 1), ("cur", W - 1), ("typ", S - 1)):
        if np.min(d[k]) < 0 or np.max(d[k]) > hi: bad.append("range of " + k)
    for k in ("x", "w0"):
        if not np.all(np.abs(d[k].astype(np.float32)) < 2.0 ** 60): bad.append("size of " + k)
    return bad
def reference(x, nxt, mem, fro, cur, typ, w0):
    pick = np.take_along_axis
    X = x.astype(np.float32).reshape(N, 8, 16, W); w = w0.astype(np.float32).reshape(N, 8, 16, K)
    nx = nxt.astype(np.int64); mb = mem.astype(np.int64); fo = fro.astype(np.int64)
    c = np.stack([gentries(a) for a in cur]).astype(np.int64).reshape(N, 8, S, K); s = np.stack([gentries(a) for a in typ]).astype(np.int64)
    for t in range(RO):
        for q in range(FI):
            at = pick(c, s[:, :, None, :], 2)[:, :, 0]
            m = pick(nx, s * W + at, 2)
            hit = np.add.reduce((pick(X, m[:, :, None, :], 3) >= w).astype(np.int64), axis=2) >= 9
            bits = pick(mb, m, 2)
            for i in range(S): c[:, :, i] = np.where((s == i) | (hit & (((bits >> i) & 1) == 1)), m, c[:, :, i])
            s = np.where(hit, np.where(s == S - 1, 0, s + 1), s)
        z = np.where(s == S - 1, 0, s + 1)
        m = pick(c, s[:, :, None, :], 2)[:, :, 0]; e = pick(c, z[:, :, None, :], 2)[:, :, 0]
        want = (((pick(mb, m, 2) >> z) & 1) == 1) & (m != e)
        slot = want & (np.add.accumulate(want.astype(np.int64), axis=2) <= CAP)
        for a in range(N):
            for g in range(8):
                j = np.nonzero(slot[a, g])[0]
                p1 = z[a, g, j] * W + m[a, g, j]; p2 = z[a, g, j] * W + e[a, g, j]
                named = np.bincount(np.concatenate([p1, p2]), minlength=S * W)
                ok = (named[p1] == 1) & (named[p2] == 1); p1 = p1[ok]; p2 = p2[ok]
                v1 = nx[a, g, p1]; v2 = nx[a, g, p2]
                nx[a, g, p1] = v2; nx[a, g, p2] = v1
        k = pick(fo, m, 2)
        y = np.stack([pick(X[(a + 1 + t) % N], k[a][:, None, :], 2) for a in range(N)])
        w = w + np.minimum(np.maximum(y - w, np.float32(-8)), np.float32(8))
    return {"yc": np.stack([gtable(a.reshape(8, S * K)) for a in c]).astype(np.float32), "yw": w.reshape(N, 128, K).astype(np.float32), "yn": nx.astype(np.float32)}

@@ -1,0 +1,543 @@
+from concourse.mybir import AluOpType as A, ActivationFunctionType as AF
+
+ROUNDS, FINDS, W, K = 3, 6, 4096, 2048
+DUMP = 3 * W
+B, FL, IN, U16, SB = "bfloat16", "float32", "int32", "uint16", "sbuf"
+rNA, rNB, rND, rV, rJB, rJD, rFR, rS, rDL, rONE = 0, 2, 4, 6, 8, 9, 10, 12, 13, 14
+
+SCRATCH = {}
+for _dt, _names in (
+    (B, "X:12288 TB:12544 xb0:4096 xb1:4096 xb2:4096 TG:2048 C2:2048 D2:2048 CM0:1024 CM1:1024 SW:4096 NL:768 NH:768 MJ:768 FB:512 VB:512 "
+        "HM0:128 HM1:128 WT:128 INC:128 A1:128 A2:128 A3:128 ON:128 WF:64 WL:64 WB:64 WR:64 XW2:16 PMX:256 PB:2048 EQ:4096 G3:256 G4:256 G5:256 YL:768 YH:768"),
+    (FL, "w:2048 D0:512 D1:512 DD0:512 DD1:512 DD2:512 DD3:512 ya:256 yb:256 CF:384 EQ3:384 PR:384 PS:128 u0:128 u1:128 p0:64 p1:64 q0:128 q1:128 "
+         "ZA0:132 ZA1:132 ZB0:132 ZB1:132 ZC0:132 ZC1:132 ZD0:132 ZD1:132 NE:128 XW:128 PIf:8 COF:512 GM:8 RM:16 RMX:256 BDm:128 IDn:128 A1f:128 A2f:128 "
+         "J2:128 J2r:128 NJ:128 RS:128 WC:64 PG:16 OW:256 OK:128 Y:256 YK:256 KD:2 DL:16 LPf:16 YC:384 CE:384 YF:768 YG:768"),
+    (IN, "NX:768 NI:768 ME:256 MI:768 FR:256 FI:512 VI:256 VH:256 VJ:512 CU:384 TY:128 ST0:192 ST1:192 CD0:128 CD1:128 PIi:4 COL:128 CO2:384 RSi:128 CY:384 TYY:384"),
+    (U16, "LA:128 LB:128 LD:128 LK:128 LO:128 LP:16"),
+):
+    for _n in _names.split():
+        SCRATCH[_n.split(":")[0]] = (SB, [128, int(_n.split(":")[1])], _dt)
+for _n in "tb0 tb1 cb0 cb1 lb0 lb1 pa pb".split():
+    SCRATCH[_n] = ("psum", [128, 512], FL)
+GROUPS = "ldx0 ldw ldn ldm ldf ldc r1 r2 r3 r4 r5 r6 r7 r8 wa00 wa01 wa10 wa11 wa20 wa21 mg0 mg1 mg2 rb0 rb1 out1 out2 out3 yl".split()
+SEMAPHORES = ["qv", "qs", "qt", "qg", "xs", "x0", "x1", "x2"] + GROUPS
+
+
+def rank_program(g, core, T, topo):
+    rank = T.rank_of(core)
+    if rank is None:
+        return
+    Q = {"v": g.vector, "s": g.scalar, "t": g.tensor, "g": g, "y": g.sync}
+    V, S, P = g.vector, g.scalar, g.tensor
+    SEMOF = {"v": "qv", "s": "qs", "t": "qt", "g": "qg"}
+    count, known, clock, acc, closed = {}, {q: {} for q in Q}, {}, {}, {}
+
+    def r(name, c0, c1, step=1, p0=0, p1=128, ps=1):
+        return (name, c0, c1, step, p0, p1, ps)
+
+    def ap(k):
+        if k[6] != 1:
+            return T[k[0]][k[4]:k[5]:k[6], k[1]:k[2]]
+        if k[3] != 1:
+            return T[k[0]][k[4]:k[5], k[1]:k[2]:k[3]]
+        return T[k[0]][k[4]:k[5], k[1]:k[2]]
+
+    def psum(n):
+        return SCRATCH[n][0] == "psum"
+
+    def meet(a, b):
+        if a[1] >= b[2] or b[1] >= a[2] or a[4] >= b[5] or b[4] >= a[5]:
+            return False
+        if a[6] == 16 and b[6] == 16 and a[4] % 16 != b[4] % 16:
+            return False
+        if a[3] == b[3] and a[3] > 1 and (a[1] - b[1]) % a[3]:
+            return False
+        return True
+
+    def cover(a, b):
+        return a[3] == 1 and a[6] == 1 and a[1] <= b[1] and a[2] >= b[2] and a[4] <= b[4] and a[5] >= b[5]
+
+    def wait(q, ev):
+        sem, n = ev
+        if sem in GROUPS:
+            n = count[sem]
+            closed[sem] = True
+        if known[q].get(sem, 0) >= n:
+            return
+        Q[q].wait_ge(T.sem[sem], n)
+        known[q][sem] = n
+        for k2, n2 in clock.get((sem, n), {}).items():
+            if known[q].get(k2, 0) < n2:
+                known[q][k2] = n2
+
+    def deps(q, reads, writes):
+        best = {}
+        for isw, lst in ((False, reads), (True, writes)):
+            for k in lst:
+                for (k2, w2, ev, q2) in acc.get(k[0], []):
+                    if psum(k[0]):
+                        if q2 == q and (q == "t" or not (isw or w2) or not meet(k, k2)):
+                            continue
+                    elif not ((isw or w2) and meet(k, k2)):
+                        continue
+                    best[ev[0]] = max(best.get(ev[0], 0), ev[1])
+        for s_ in sorted(best):
+            wait(q, (s_, best[s_]))
+
+    def note(q, reads, writes, ev, dma):
+        tag = "dma" if dma else q
+        for isw, lst in ((False, reads), (True, writes)):
+            for k in lst:
+                old = acc.get(k[0], [])
+                if psum(k[0]):
+                    old = [o for o in old if o[3] == tag and o[0] != k]
+                    if isw and tag != "t":
+                        old = [o for o in old if not cover(k, o[0])]
+                elif isw:
+                    old = [o for o in old if not cover(k, o[0])]
+                elif not dma:
+                    old = [o for o in old if not (o[3] == tag and not o[1] and o[0] == k)]
+                acc[k[0]] = old + [(k, isw, ev, tag)]
+
+    def op(q, fn, reads, writes):
+        deps(q, reads, writes)
+        sem = SEMOF[q]
+        count[sem] = count.get(sem, 0) + 1
+        ev = (sem, count[sem])
+        fn().then_inc(T.sem[sem], 1)
+        c = dict(known[q])
+        c[sem] = count[sem]
+        clock[ev] = c
+        note(q, reads, writes, ev, False)
+
+    def dma(q, grp, out, in_, outk=None, ink=None):
+        assert not closed.get(grp)
+        rd, wr = [ink] if ink else [], [outk] if outk else []
+        deps(q, rd, wr)
+        count[grp] = count.get(grp, 0) + 16
+        Q[q].dma_start(out, in_).then_inc(T.sem[grp], 16)
+        note(q, rd, wr, (grp, 0), True)
+
+    def mv(q, grp, o, i):
+        dma(q, grp, ap(o), ap(i), o, i)
+
+    def add(grp, o, i):
+        deps("g", [i], [o])
+        count[grp] = count.get(grp, 0) + 16
+        g.dma_start(ap(o), ap(i), accum_op=A.add).then_inc(T.sem[grp], 16)
+        note("g", [i], [o], (grp, 0), True)
+
+    def tt(o, a, b, f):
+        op("v", lambda: V.tensor_tensor(ap(o), ap(a), ap(b), f), [a, b], [o])
+
+    def ts(o, a, s1, f, s2=None, f2=None):
+        rd = [a] + [k for k in (s1, s2) if isinstance(k, tuple)]
+        x1 = ap(s1) if isinstance(s1, tuple) else s1
+        x2 = ap(s2) if isinstance(s2, tuple) else s2
+        if f2 is None:
+            op("v", lambda: V.tensor_scalar(ap(o), ap(a), x1, None, f), rd, [o])
+        else:
+            op("v", lambda: V.tensor_scalar(ap(o), ap(a), x1, x2, f, f2), rd, [o])
+
+    def cp(o, a):
+        op("v", lambda: V.tensor_copy(ap(o), ap(a)), [a], [o])
+
+    def mset(o, c):
+        op("v", lambda: V.memset(ap(o), c), [], [o])
+
+    def mm(o, l, h, start, stop):
+        op("t", lambda: P.matmul(ap(o), ap(l), ap(h), start, stop), [l, h], [o])
+
+    def act(o, a, f, bias=0.0, scale=1.0):
+        b = ap(bias) if isinstance(bias, tuple) else bias
+        op("s", lambda: S.activation(ap(o), ap(a), f, b, scale), [a] + ([bias] if isinstance(bias, tuple) else []), [o])
+
+    def sca(o, a, c):
+        op("s", lambda: S.activation(ap(o), ap(a), AF.Copy, 0.0, ap(c)), [a, c], [o])
+
+    def look(q, o, win, off):
+        if q == "v":
+            op("v", lambda: V.tensor_copy(ap(o), ap(win).indirect(ap(off))), [win, off], [o])
+        else:
+            op("s", lambda: S.activation(ap(o), ap(win).indirect(ap(off)), AF.Copy), [win, off], [o])
+
+    def iota(o, pat, base, cm):
+        op("g", lambda: g.iota(ap(o), pat, base, cm), [], [o])
+
+    dma("y", "ldn", T.NX[:, :], T.nxt[:, :], r("NX", 0, 768))
+    dma("s", "ldx0", T.X[:, 0:W], T.x[:, :], r("X", 0, W))
+    dma("y", "ldm", T.ME[:, :], T.mem[:, :], r("ME", 0, 256))
+    dma("y", "ldf", T.FR[:, :], T.fro[:, :], r("FR", 0, 256))
+    dma("y", "ldc", T.CU[:, :], T.cur[:, :], r("CU", 0, 384))
+    dma("y", "ldc", T.TY[:, :], T.typ[:, :], r("TY", 0, 128))
+    dma("s", "ldw", T.C2[:, :], T.w0[:, :], r("C2", 0, K))
+    iota(r("PIi", 0, 1), [[1, 1]], 0, 1)
+    iota(r("COL", 0, 128), [[1, 128]], 0, 0)
+    iota(r("VI", 0, 256), [[1, 256]], 0, 256)
+    iota(r("RSi", 0, 128), [[0, 16], [1, 8]], 0, 0)
+    for h in range(2):
+        op("g", lambda: g.iota(T.J2r[:, 64 * h:64 * h + 64], [[0, 8], [2, 8]], 2048 + 1024 * h, 16, allow_small_or_imprecise_dtypes=True), [], [r("J2r", 64 * h, 64 * h + 64)])
+
+    wait("g", ("ldx0", 0))
+    nloc = 0
+    for t in range(ROUNDS):
+        dst = T.cores[(rank - 1 - t) % len(T.cores)]
+        rid, pid, _se = topo.addr(dst)
+        g.remote_dma(T["xb%d" % t][:, :], T.X[:, 0:W], T.sem["x%d" % t], T.sem.xs, pid, rid, topo.mask(core, dst))
+        nloc += len(topo.engines(core, dst))
+        src = T.cores[(rank + 1 + t) % len(T.cores)]
+        count["x%d" % t] = len(topo.engines(src, core))
+        acc["xb%d" % t] = [(r("xb%d" % t, 0, W), True, ("x%d" % t, count["x%d" % t]), "dma")]
+
+    ts(r("PIi", 1, 2), r("PIi", 0, 1), 4, A.logical_shift_right)
+    ts(r("PIi", 2, 3), r("PIi", 0, 1), 15, A.bitwise_and)
+    ts(r("PIi", 3, 4), r("PIi", 0, 1), 63, A.bitwise_and)
+    cp(r("COF", 0, 128), r("COL", 0, 128))
+    cp(r("PIf", 0, 4), r("PIi", 0, 4))
+    pP, pG, pR, pC = (r("PIf", i, i + 1) for i in range(4))
+    cC, cG, cR, cQ = (r("COF", 128 * i, 128 * i + 128) for i in range(4))
+    ts(r("GM", 0, 8), r("COF", 0, 8), pG, A.is_equal)
+    ts(r("RM", 0, 16), r("COF", 0, 16), pR, A.is_equal)
+    cols = {}
+
+    def col(*terms):
+        key = ()
+        for (rw, wt) in terms:
+            prev = cols.get(key)
+            key = key + ((rw, wt),)
+            if key not in cols:
+                n = len(cols)
+                o = r("WC", n, n + 1)
+                if prev is None:
+                    ts(o, r("RM", rw, rw + 1), float(wt), A.mult)
+                else:
+                    ts(o, r("RM", rw, rw + 1), float(wt), A.mult, prev, A.add)
+                cols[key] = o
+        return cols[key]
+
+    def num(a, f=1):
+        return ((a, f), (a + 1, 64 * f))
+
+    def trow(rw, c0, c1):
+        return r("TB", c0, c1, 1, rw, 128, 16)
+
+    def rebuild(grp):
+        n = 0
+        for i in range(2):
+            for d0, d1, s0, a in ((0, 2 * W, W, 1), (2 * W, 3 * W, 0, 1), (0, W, 2 * W, 2), (W, 3 * W, 0, 2)):
+                mv("ys"[n % 2], grp, trow(2 * a + i, d0, d1), trow(i, s0, s0 + d1 - d0))
+                n += 1
+
+    def fill(s):
+        fc = col((rS, s), (rDL, 1 if s < 2 else -2), (rONE, 1))
+        if s < 2:
+            ts(r("TB", W * s, W * s + W), r("X", 0, W), 0.0, A.mult, fc, A.add)
+        else:
+            act(r("TB", W * s, W * s + W), r("X", 0, W), AF.Identity, fc, 0.0)
+
+    ts(r("NI", 0, 768), r("NX", 0, 768), 63, A.bitwise_and)
+    cp(r("NL", 0, 768), r("NI", 0, 768))
+    ts(r("VH", 0, 256), r("VI", 0, 256), 4095, A.bitwise_and)
+    ts(r("NI", 0, 768), r("NX", 0, 768), 6, A.logical_shift_right)
+    cp(r("NH", 0, 768), r("NI", 0, 768))
+    for s in range(3):
+        fill(s)
+    mv("y", "r1", trow(rNA, 0, 3 * W), r("NL", 0, 768))
+    mv("s", "r2", trow(rNA + 1, 0, 3 * W), r("NH", 0, 768))
+    ts(r("VJ", 0, 256), r("VH", 0, 256), 63, A.bitwise_and)
+    ts(r("VJ", 256, 512), r("VH", 0, 256), 6, A.logical_shift_right)
+    cp(r("VB", 0, 512), r("VJ", 0, 512))
+    ts(r("FI", 0, 256), r("FR", 0, 256), 63, A.bitwise_and)
+    ts(r("FI", 256, 512), r("FR", 0, 256), 6, A.logical_shift_right)
+    cp(r("FB", 0, 512), r("FI", 0, 512))
+    for i in range(3):
+        ts(r("MI", 256 * i, 256 * i + 256), r("ME", 0, 256), i, A.logical_shift_right, 1, A.bitwise_and)
+    ts(r("MJ", 0, 768), r("MI", 0, 768), -1.0, A.mult, 1.0, A.add)
+    mset(r("TB", DUMP, DUMP + 256), 0.0)
+    for i in range(2):
+        mv("y", "r3", trow(rV + i, 0, W), r("VB", 256 * i, 256 * i + 256))
+    rebuild("r5")
+    for s in (0, 1):
+        for i in range(2):
+            mv("s", "r6", trow(rV + i, W * s + W, W * s + 2 * W), trow(rV + i, 0, W))
+    for i in range(2):
+        mv("y", "r4", trow(rFR + i, 0, W), r("FB", 256 * i, 256 * i + 256))
+    for s in range(3):
+        mv("y", "r7", trow(rJB, W * s, W * s + W), r("MJ", 256 * ((s + 1) % 3), 256 * ((s + 1) % 3) + 256))
+    for s in (0, 1):
+        for i in range(2):
+            mv("s", "r6", trow(rFR + i, W * s + W, W * s + 2 * W), trow(rFR + i, 0, W))
+    mv("y", "r8", trow(rJD, 0, 2 * W), trow(rJB, W, 3 * W))
+    mv("y", "r8", trow(rJD, 2 * W, 3 * W), trow(rJB, 0, W))
+    for s in (1, 2):
+        act(r("X", W * s, W * s + W), r("X", 0, W), AF.Copy)
+    act(r("w", 0, K), r("C2", 0, K), AF.Copy)
+
+    for i in range(3):
+        ts(r("EQ3", 128 * i, 128 * i + 128), r("TY", 0, 128), float(i), A.is_equal)
+        ts(r("CF", 128 * i, 128 * i + 128), r("CU", 128 * i, 128 * i + 128), float(W * i), A.add)
+    for n, L in enumerate(("LA", "LB", "LD")):
+        for i in range(3):
+            e = (i - n) % 3
+            tt(r("PR", 128 * i, 128 * i + 128), r("CF", 128 * i, 128 * i + 128), r("EQ3", 128 * e, 128 * e + 128), A.mult)
+        tt(r("PS", 0, 128), r("PR", 0, 128), r("PR", 128, 256), A.add)
+        tt(r("PS", 0, 128), r("PS", 0, 128), r("PR", 256, 384), A.add)
+        cp(r(L, 0, 128), r("PS", 0, 128))
+
+    ts(r("CO2", 0, 128), r("COL", 0, 128), 4, A.logical_shift_right)
+    ts(r("CO2", 128, 256), r("COL", 0, 128), 15, A.bitwise_and)
+    ts(r("CO2", 256, 384), r("COL", 0, 128), 63, A.bitwise_and)
+    cp(r("COF", 128, 512), r("CO2", 0, 384))
+    ts(r("RMX", 0, 128), cR, pR, A.is_equal)
+    ts(r("RMX", 128, 256), cR, pR, A.is_equal)
+    ts(r("BDm", 0, 128), cG, pG, A.is_equal)
+    ts(r("IDn", 0, 128), cC, pP, A.is_equal)
+    ts(r("A1f", 0, 128), cQ, pC, A.is_equal)
+    cp(r("A1", 0, 128), r("A1f", 0, 128))
+    ts(r("A2f", 0, 128), cC, pP, A.is_ge)
+    tt(r("A2f", 0, 128), r("A2f", 0, 128), r("A1f", 0, 128), A.mult)
+    tt(r("A2", 0, 128), r("A2f", 0, 128), r("A1f", 0, 128), A.subtract)
+    ts(r("A3", 0, 128), cQ, pC, A.is_gt)
+    mset(r("ON", 0, 128), 1.0)
+    ts(r("PIf", 4, 5), pP, 64.0, A.is_ge, -1023.0, A.mult)
+    ts(r("J2", 0, 128), r("J2r", 0, 128), r("PIf", 4, 5), A.add)
+    ts(r("NJ", 0, 128), r("J2", 0, 128), -1.0, A.mult, -1.0, A.add)
+    ts(r("RS", 0, 128), r("RSi", 0, 128), 0.0, A.is_gt)
+    ts(r("KD", 0, 1), pP, -1.0, A.mult, 16384.0 - DUMP, A.add)
+    ts(r("KD", 1, 2), pP, -1.0, A.mult, 16384.0 - DUMP - 128, A.add)
+    ts(r("DL", 0, 16), r("COF", 0, 16), 16.0, A.mult, float(DUMP), A.add)
+    ts(r("DL", 0, 16), r("DL", 0, 16), pR, A.add)
+    for z in ("ZA0", "ZA1", "ZB0", "ZB1", "ZC0", "ZC1", "ZD0", "ZD1"):
+        mset(r(z, 0, 132), 0.0)
+
+    def wblock(buf, i, *terms):
+        sca(r(buf, 8 * i, 8 * i + 8), r("GM", 0, 8), col(*terms))
+
+    s4 = (rS, W)
+    packA = num(rV, W) + num(rNA)
+    packD = num(rV, W) + num(rND)
+    nextA = (s4,) + num(rNA)
+    for i, c in enumerate((packA, nextA)):
+        wblock("WR", i, *c)
+    minusA = ((rNA, -1), (rNA + 1, -64))
+    for i, c in enumerate((num(rNB), packD, ((rJB, 1),), ((rJD, 1),), minusA + num(rNB) + ((rDL, W),), packD, packA, nextA)):
+        wblock("WF", i, *c)
+    for i, c in enumerate((num(rV), packD, ((rJB, 1),), ((rJD, 1),), ((rDL, W),), packD, packA, num(rV) + (s4,))):
+        wblock("WL", i, *c)
+    for i in range(2):
+        cp(r("XW2", 8 * i, 8 * i + 8), r("GM", 0, 8))
+    for i, c in enumerate((num(rV), ((rONE, 1), (rJB, -1)), (s4, (rDL, W)), ((rONE, 3 * W), (rS, -2 * W), (rDL, -W)), num(rFR))):
+        wblock("WB", i, *c)
+    for i, c in enumerate((num(rNB), num(rV))):
+        pc = col(*(c + (s4, (rONE, -16384))))
+        sca(r("PG", 8 * i, 8 * i + 8), r("GM", 0, 8), pc)
+        sca(r("PMX", 128 * i, 128 * i + 128), r("BDm", 0, 128), pc)
+        for g_ in range(8):
+            sca(r("PB", 256 * g_ + 128 * i, 256 * g_ + 128 * i + 128), r("ON", 0, 128), r("PG", 8 * i + g_, 8 * i + g_ + 1))
+    isn = col((rNA, 1), (rNA + 1, 1))
+    ts(r("PIf", 5, 6), isn, -1.0, A.mult, 1.0, A.add)
+
+    def units(ps, src, c0, wbuf, n):
+        for b in range(16):
+            k, e = b // 2, b % 2
+            mm(r(ps, k, 64 * n, 8, 64 * e, 64 * e + 64), r(src, c0 + b, c0 + 1024, 16), r(wbuf, 0, 8 * n), True, True)
+
+    def zc(z):
+        return r(z, 1, 129, 2)
+
+    def mklist(z, ps, pc, dst, h):
+        mm(r(ps, pc, pc + 64), r(z, 1, 129), r("IDn", 0, 64), True, False)
+        mm(r(ps, pc, pc + 64), r(z, 0, 128), r("IDn", 64, 128), False, True)
+        return lambda: cp(r(dst, 64 * h, 64 * h + 64), r(ps, pc, pc + 64))
+
+    TBw = r("TB", 0, DUMP + 256)
+
+    def refresh():
+        def ask(n, buf, L):
+            for h in range(2):
+                look("vs"[(h + n) % 2], r(buf, 1024 * h, 1024 * h + 1024), TBw, r(L, 64 * h, 64 * h + 64))
+        ask(0, "TG", "LA")
+        ask(1, "C2", "LB")
+        fin = []
+        for h in range(2):
+            units("tb%d" % h, "TG", 1024 * h, "WR", 2)
+            cp(zc("ZA%d" % h), r("tb%d" % h, 64, 128))
+            fin.append(mklist("ZA%d" % h, "lb%d" % h, 0, "LA", h))
+            units("cb%d" % h, "C2", 1024 * h, "WR", 1)
+        for f in fin:
+            f()
+        gath(0)
+        ask(2, "D2", "LD")
+        gath(1)
+        for h in range(2):
+            st, pd = "ST%d" % h, ("pa", "pb")[h]
+            cp(r(st, 128, 192), r("cb%d" % h, 0, 64))
+            units(pd, "D2", 1024 * h, "WR", 1)
+            ts(r(st, 0, 64), r(st, 128, 192), 4095, A.bitwise_and)
+            cp(r(st, 64, 128), r(pd, 0, 64))
+
+    def gath(h):
+        off = r("LA", 64 * h, 64 * h + 64)
+        xw, cm, wv = r("X", 0, 3 * W), r("CM%d" % h, 0, 1024), r("w", 1024 * h, 1024 * h + 1024)
+        look("s", r("TG", 1024 * h, 1024 * h + 1024), TBw, off)
+        op("v", lambda: V.tensor_tensor(ap(cm), ap(xw).indirect(ap(off)), ap(wv), A.is_ge), [xw, off, wv], [cm])
+
+    def update(h, last):
+        tb, cb, st, u, q, p, hm, z = ("%s%d" % (n, h) for n in ("tb", "cb", "ST", "u", "q", "p", "HM", "ZA"))
+        sl = lambda a, b: r(tb, 64 * a, 64 * b)
+        units(tb, "TG", 1024 * h, "WL" if last else "WF", 8)
+        units(cb, "CM%d" % h, 0, "XW2", 2)
+        if last:
+            ts(r(st, 0, 64), r(st, 128, 192), 12, A.logical_shift_right)
+        dl = ("pa", "pb")[h]
+        tt(r(u, 0, 128), r(st, 0, 128), sl(0, 2), A.subtract)
+        tt(r(dl, 0, 64), sl(6, 7), r(st, 64, 128), A.subtract)
+        tt(r(q, 0, 128), r(u, 0, 128), sl(2, 4), A.mult)
+        tt(sl(0, 2), r(q, 0, 128), sl(4, 6), A.add)
+        tt(r(dl, 64, 128), sl(1, 2), r(st, 128, 192), A.subtract)
+        act(r(hm, 0, 128), r(cb, 0, 128), AF.Sigmoid, -3400.0, 400.0)
+        tt(r(p, 0, 64), sl(0, 1), r(hm, 0, 64), A.mult)
+        tt(zc(z), r(p, 0, 64), sl(7, 8), A.add)
+        fin = mklist(z, "lb%d" % h, 0, "LA", h)
+        tt(r(dl, 0, 128), r(dl, 0, 128), r(hm, 0, 128), A.mult)
+        tt(r(st, 64, 192), r(st, 64, 192), r(dl, 0, 128), A.add)
+        if not last:
+            ts(r(st, 0, 64), r(st, 128, 192), 4095, A.bitwise_and)
+        fin()
+
+    def finds():
+        for q in range(FINDS):
+            for h in range(2):
+                update(h, q == FINDS - 1)
+                if q < FINDS - 1:
+                    gath(h)
+
+    def boundary(t):
+        for h in range(2):
+            look("vs"[h], r("TG", 1024 * h, 1024 * h + 1024), TBw, r("LA", 64 * h, 64 * h + 64))
+        for h in range(2):
+            ts(r("CD%d" % h, 0, 128), r("ST%d" % h, 64, 192), 12, A.logical_shift_right)
+            units("tb%d" % h, "TG", 1024 * h, "WB", 5)
+        mset(r("SW", 0, 128), 0.0)
+        fin = []
+        for h in range(2):
+            tb, cd = "tb%d" % h, "CD%d" % h
+            tt(zc("ZA%d" % h), r(tb, 128, 192), r(cd, 64, 128), A.add)
+            fin.append(mklist("ZA%d" % h, "lb%d" % h, 0, "LB", h))
+            tt(r("NE", 64 * h, 64 * h + 64), r(tb, 0, 64), r(cd, 64, 128), A.not_equal)
+            tt(r("WT", 64 * h, 64 * h + 64), r(tb, 64, 128), r("NE", 64 * h, 64 * h + 64), A.mult)
+        for f in fin:
+            f()
+        for h in range(2):
+            look("s", r("C2", 1024 * h, 1024 * h + 1024), TBw, r("LB", 64 * h, 64 * h + 64))
+        for i in range(2):
+            mv("y", "mg%d" % t, r("C2", 0, K, 1, rNB + i, 128, 16), r("TG", 0, K, 1, rV + i, 128, 16))
+        op("v", lambda: V.tensor_tensor_scan(T.INC[:, :], T.RS[:, :], T.WT[:, :], 0.0, A.mult, A.add), [r("RS", 0, 128), r("WT", 0, 128)], [r("INC", 0, 128)])
+        for h in range(2):
+            c = 64 * h
+            mm(r("pa", c, c + 64), r("IDn", 0, 128), r("NJ", c, c + 64), True, False)
+            mm(r("pa", c, c + 64), r("A2", 0, 128), r("WT", c, c + 64), False, False)
+            mm(r("pa", c, c + 64), r("A1", 0, 128), r("INC", c, c + 64), False, False)
+            for k in range(8):
+                if h:
+                    mm(r("pa", c + k, c + 64, 8), r("ON", 0, 128), r("INC", 7, 64, 8), False, False)
+                mm(r("pa", c + k, c + 64, 8), r("A3", 0, 128), r("INC", c + 7, c + 64, 8), False, k == 7)
+        tt(r("XW", 0, 128), r("pa", 0, 128), r("WT", 0, 128), A.mult)
+        fin = []
+        for h in range(2):
+            c = 64 * h
+            tt(zc("ZD%d" % h), r("XW", c, c + 64), r("J2", c, c + 64), A.add)
+            fin.append(mklist("ZD%d" % h, "cb%d" % h, 0, "LO", h))
+        for f in fin:
+            f()
+        fin = []
+        for h in range(2):
+            tb, cd = "tb%d" % h, "CD%d" % h
+            cp(zc("ZC%d" % h), r(tb, 256, 320))
+            fin.append(mklist("ZC%d" % h, "lb%d" % h, 0, "LK", h))
+            tt(zc("ZB%d" % h), r(tb, 192, 256), r(cd, 0, 64), A.add)
+            fin.append(mklist("ZB%d" % h, "lb%d" % h, 64, "LD", h))
+        for f in fin:
+            f()
+        pull(t, 0, 2)
+        op("v", lambda: V.tensor_copy(T.SW[:, 0:4096].indirect(T.LO[:, 0:128]), T.C2[:, :]), [r("C2", 0, K), r("LO", 0, 128)], [r("SW", 0, 4096)])
+        SWs = r("SW", 0, 128)
+        for i in range(2):
+            mm(r("pb", 128 * i, 128 * i + 128), SWs, r("PMX", 128 * i, 128 * i + 128), True, True)
+        cp(r("OW", 0, 256), r("pb", 0, 256))
+        banks = ("cb0", "cb1", "lb0", "lb1")
+        order = (4, 6, 0, 1, 7, 2, 3, 5)
+        for g_ in range(8):
+            b, o = banks[g_ // 2], 256 * (g_ % 2)
+            for i in range(2):
+                mm(r(b, o + 128 * i, o + 128 * i + 128), r("PB", 256 * g_ + 128 * i, 256 * g_ + 128 * i + 128), SWs, True, True)
+        for g_ in order:
+            b, o = banks[g_ // 2], 256 * (g_ % 2)
+            for i in range(2):
+                e, own = r("EQ", 512 * g_ + 256 * i, 512 * g_ + 256 * i + 256), r("OW", 128 * i + 16 * g_, 128 * i + 16 * g_ + 1)
+                if g_ < 5:
+                    ts(e, r(b, o, o + 256), own, A.is_equal)
+                else:
+                    y = r(("ya", "yb")[i], 0, 256)
+                    act(y, r(b, o, o + 256), AF.Abs, own, -1.0)
+                    act(e, y, AF.Relu, 1.0, -1.0)
+        for g_ in order:
+            for i in range(4):
+                mm(r("pa", 16 * g_, 16 * g_ + 16), r("EQ", 512 * g_ + 128 * i, 512 * g_ + 128 * i + 128), r("ON", 0, 16), i == 0, i == 3)
+        for i in range(2):
+            ts(r("Y", 128 * i, 128 * i + 128), r("OW", 128 * i, 128 * i + 128), r("KD", i, i + 1), A.add)
+        tt(r("Y", 0, 256), r("Y", 0, 256), r("RMX", 0, 256), A.mult)
+        ts(r("OK", 0, 128), r("pa", 0, 128), 2.5, A.is_le)
+        for i in range(2):
+            tt(r("YK", 128 * i, 128 * i + 128), r("Y", 128 * i, 128 * i + 128), r("OK", 0, 128), A.mult)
+            mm(r("pb", 8 * i, 8 * i + 8), r("YK", 128 * i, 128 * i + 128), r("GM", 0, 8), True, True)
+        tt(r("LPf", 0, 16), r("pb", 0, 16), r("DL", 0, 16), A.add)
+        cp(r("LP", 0, 16), r("LPf", 0, 16))
+        look("v", r("G3", 0, 256), TBw, r("LP", 0, 16))
+        ts(r("G4", 0, 256), r("G3", 0, 256), r("PIf", 5, 6), A.mult)
+        ts(r("G5", 0, 128), r("G3", 128, 256), isn, A.mult)
+        ts(r("G5", 128, 256), r("G3", 0, 128), isn, A.mult)
+        tt(r("G4", 0, 256), r("G4", 0, 256), r("G5", 0, 256), A.add)
+        op("v", lambda: V.tensor_copy(ap(TBw).indirect(T.LP[:, 0:16]), T.G4[:, :]), [r("G4", 0, 256), r("LP", 0, 16)], [TBw])
+        if t < ROUNDS - 1:
+            rebuild("rb%d" % t)
+        else:
+            for i, d in ((0, "YL"), (1, "YH")):
+                mv("ys"[i], "yl", r(d, 0, 768), trow(i, 0, 3 * W))
+        pull(t, 2, 4)
+
+    def pull(t, c0, c1):
+        xb = r("xb%d" % t, 0, W)
+        for c in range(c0, c1):
+            d, wv = r("D%d" % (c % 2), 0, 512), r("w", 512 * c, 512 * c + 512)
+            off, cl = r("LK", 32 * c, 32 * c + 32), r("DD%d" % c, 0, 512)
+            op("v", lambda: V.tensor_tensor(ap(d), ap(xb).indirect(ap(off)), ap(wv), A.subtract), [xb, off, wv], [d])
+            ts(cl, d, -8.0, A.max, 8.0, A.min)
+            add("wa%d%d" % (t, c // 2), wv, cl)
+
+    refresh()
+    for t in range(ROUNDS):
+        finds()
+        boundary(t)
+        if t < ROUNDS - 1:
+            refresh()
+    dma("y", "out1", T.yw[:, :], T.w[:, :], None, r("w", 0, K))
+    for i, L in enumerate(("LA", "LB", "LD")):
+        cp(r("CY", 128 * i, 128 * i + 128), r(L, 0, 128))
+    ts(r("TYY", 0, 384), r("CY", 0, 384), 12, A.logical_shift_right)
+    ts(r("CY", 0, 384), r("CY", 0, 384), 4095, A.bitwise_and)
+    for i in range(3):
+        ts(r("CE", 0, 384), r("TYY", 0, 384), float(i), A.is_equal)
+        tt(r("PR", 0, 384), r("CE", 0, 384), r("CY", 0, 384), A.mult)
+        tt(r("PS", 0, 128), r("PR", 0, 128), r("PR", 128, 256), A.add)
+        tt(r("YC", 128 * i, 128 * i + 128), r("PS", 0, 128), r("PR", 256, 384), A.add)
+    dma("y", "out2", T.yc[:, :], T.YC[:, :], None, r("YC", 0, 384))
+    ts(r("YG", 0, 768), r("YH", 0, 768), 64.0, A.mult)
+    tt(r("YF", 0, 768), r("YG", 0, 768), r("YL", 0, 768), A.add)
+    dma("y", "out3", T.yn[:, :], T.YF[:, :], None, r("YF", 0, 768))
+    for sem in SEMAPHORES:
+        if sem == "xs":
+            g.wait_ge(T.sem.xs, nloc)
+        elif count.get(sem, 0):
+            known["g"].pop(sem, None)
+            wait("g", (sem, count[sem]))

@@ -7,19 +7,20 @@ rNA, rNB, rND, rV, rJB, rJD, rFR, rS, rDL, rONE = 0, 2, 4, 6, 8, 9, 10, 12, 13, 
 
 SCRATCH = {}
 for _dt, _names in (
-    (B, "X:12288 TB:12544 xb0:4096 xb1:4096 xb2:4096 TG:2048 C2:2048 D2:2048 CM0:1024 CM1:1024 SW:4096 NL:768 NH:768 MJ:768 FB:512 VB:512 "
-        "HM0:128 HM1:128 WT:128 INC:128 A1:128 A2:128 A3:128 ON:128 WF:64 WL:64 WB:64 WR:64 XW2:16 PMX:256 PB:2048 EQ:4096 G3:256 G4:256 G5:256 YL:768 YH:768"),
-    (FL, "w:2048 D0:512 D1:512 DD0:512 DD1:512 DD2:512 DD3:512 ya:256 yb:256 CF:384 EQ3:384 PR:384 PS:128 u0:128 u1:128 p0:64 p1:64 q0:128 q1:128 "
-         "ZA0:132 ZA1:132 ZB0:132 ZB1:132 ZC0:132 ZC1:132 ZD0:132 ZD1:132 NE:128 XW:128 PIf:8 COF:512 GM:8 RM:16 RMX:256 BDm:128 IDn:128 A1f:128 A2f:128 "
-         "J2:128 J2r:128 NJ:128 RS:128 WC:64 PG:16 OW:256 OK:128 Y:256 YK:256 KD:2 DL:16 LPf:16 YC:384 CE:384 YF:768 YG:768"),
-    (IN, "NX:768 NI:768 ME:256 MI:768 FR:256 FI:512 VI:256 VH:256 VJ:512 CU:384 TY:128 ST0:192 ST1:192 CD0:128 CD1:128 PIi:4 COL:128 CO2:384 RSi:128 CY:384 TYY:384"),
-    (U16, "LA:128 LB:128 LD:128 LK:128 LO:128 LP:16"),
+    (B, "X:12288 TB:12544 xb0:4096 xb1:4096 xb2:4096 TG:2064 C2:2064 D2:2048 CM0:1024 CM1:1024 SM:128 SC:128 CP:1024 CP2:128 IOR:128 BDb:128 EC0:128 EC1:128 "
+        "NL:768 NH:768 MJ:768 FB:512 VB:512 HM0:128 HM1:128 WT:128 INC:128 A1:128 A2:128 A3:128 ON:128 WF:64 WL:64 WB:64 WR:64 XW2:16 PMX:256 PB:2048 EQ:4096 "
+        "G3:256 G4:256 G5:256"),
+    (FL, "w:2048 D0:512 D1:512 DD0:512 DD1:512 DD2:512 DD3:512 ya:256 yb:256 CF:384 EQ3:384 PR:384 u0:128 u1:128 p0:64 p1:64 q0:128 q1:128 "
+         "ZA0:132 ZA1:132 ZB0:132 ZB1:132 ZC0:132 ZC1:132 ZD0:132 ZD1:132 NE:128 RKW:136 CEN:8 BX:128 JX:128 GM16:8 PIf:8 COF:512 GM:8 RM:16 RMX:256 BDm:128 IDn:128 "
+         "RS:128 WC:64 PG:16 OW:256 OK:128 Y:256 YK:256 KD:2 DL:16 LPf:16 YF:768"),
+    (IN, "NX:768 NI:768 ME:256 MI:768 FR:256 FI:512 VI:256 VJ:512 CU:384 TY:128 ST0:192 ST1:192 CD0:128 CD1:128 PIi:4 COL:128 CO2:384 RSi:128"),
+    (U16, "LA:128 LB:128 LD:128 LK:128 LQ:8 LJ:8 LP:16"),
 ):
     for _n in _names.split():
         SCRATCH[_n.split(":")[0]] = (SB, [128, int(_n.split(":")[1])], _dt)
 for _n in "tb0 tb1 cb0 cb1 lb0 lb1 pa pb".split():
     SCRATCH[_n] = ("psum", [128, 512], FL)
-GROUPS = "ldx0 ldw ldn ldm ldf ldc r1 r2 r3 r4 r5 r6 r7 r8 wa00 wa01 wa10 wa11 wa20 wa21 mg0 mg1 mg2 rb0 rb1 out1 out2 out3 yl".split()
+GROUPS = "ldx0 ldw ldn ldm ldf ldc r1 r2 r3 r4 r5 r6 r7 r8 wa00 wa01 wa10 wa11 wa20 rb0 rb1 out0 out1 out2 out3 yl".split()
 SEMAPHORES = ["qv", "qs", "qt", "qg", "xs", "x0", "x1", "x2"] + GROUPS
 
 
@@ -170,13 +171,11 @@ def rank_program(g, core, T, topo):
     dma("y", "ldf", T.FR[:, :], T.fro[:, :], r("FR", 0, 256))
     dma("y", "ldc", T.CU[:, :], T.cur[:, :], r("CU", 0, 384))
     dma("y", "ldc", T.TY[:, :], T.typ[:, :], r("TY", 0, 128))
-    dma("s", "ldw", T.C2[:, :], T.w0[:, :], r("C2", 0, K))
+    dma("s", "ldw", T.C2[:, 0:K], T.w0[:, :], r("C2", 0, K))
     iota(r("PIi", 0, 1), [[1, 1]], 0, 1)
     iota(r("COL", 0, 128), [[1, 128]], 0, 0)
     iota(r("VI", 0, 256), [[1, 256]], 0, 256)
     iota(r("RSi", 0, 128), [[0, 16], [1, 8]], 0, 0)
-    for h in range(2):
-        op("g", lambda: g.iota(T.J2r[:, 64 * h:64 * h + 64], [[0, 8], [2, 8]], 2048 + 1024 * h, 16, allow_small_or_imprecise_dtypes=True), [], [r("J2r", 64 * h, 64 * h + 64)])
 
     wait("g", ("ldx0", 0))
     nloc = 0
@@ -222,30 +221,26 @@ def rank_program(g, core, T, topo):
         return r("TB", c0, c1, 1, rw, 128, 16)
 
     def rebuild(grp):
-        n = 0
         for i in range(2):
             for d0, d1, s0, a in ((0, 2 * W, W, 1), (2 * W, 3 * W, 0, 1), (0, W, 2 * W, 2), (W, 3 * W, 0, 2)):
-                mv("ys"[n % 2], grp, trow(2 * a + i, d0, d1), trow(i, s0, s0 + d1 - d0))
-                n += 1
+                mv("y", grp, trow(2 * a + i, d0, d1), trow(i, s0, s0 + d1 - d0))
 
-    def fill(s):
+    mset(r("TB", 2 * W, 3 * W + 256), 0.0)
+    for s in range(3):
         fc = col((rS, s), (rDL, 1 if s < 2 else -2), (rONE, 1))
         if s < 2:
-            ts(r("TB", W * s, W * s + W), r("X", 0, W), 0.0, A.mult, fc, A.add)
+            ts(r("TB", W * s, W * s + W), r("TB", 2 * W, 3 * W), fc, A.add)
         else:
-            act(r("TB", W * s, W * s + W), r("X", 0, W), AF.Identity, fc, 0.0)
-
+            act(r("TB", W * s, W * s + W), r("TB", W * s, W * s + W), AF.Identity, fc)
     ts(r("NI", 0, 768), r("NX", 0, 768), 63, A.bitwise_and)
     cp(r("NL", 0, 768), r("NI", 0, 768))
-    ts(r("VH", 0, 256), r("VI", 0, 256), 4095, A.bitwise_and)
+    ts(r("VI", 0, 256), r("VI", 0, 256), 4095, A.bitwise_and)
     ts(r("NI", 0, 768), r("NX", 0, 768), 6, A.logical_shift_right)
     cp(r("NH", 0, 768), r("NI", 0, 768))
-    for s in range(3):
-        fill(s)
     mv("y", "r1", trow(rNA, 0, 3 * W), r("NL", 0, 768))
-    mv("s", "r2", trow(rNA + 1, 0, 3 * W), r("NH", 0, 768))
-    ts(r("VJ", 0, 256), r("VH", 0, 256), 63, A.bitwise_and)
-    ts(r("VJ", 256, 512), r("VH", 0, 256), 6, A.logical_shift_right)
+    mv("y", "r2", trow(rNA + 1, 0, 3 * W), r("NH", 0, 768))
+    ts(r("VJ", 0, 256), r("VI", 0, 256), 63, A.bitwise_and)
+    ts(r("VJ", 256, 512), r("VI", 0, 256), 6, A.logical_shift_right)
     cp(r("VB", 0, 512), r("VJ", 0, 512))
     ts(r("FI", 0, 256), r("FR", 0, 256), 63, A.bitwise_and)
     ts(r("FI", 256, 512), r("FR", 0, 256), 6, A.logical_shift_right)
@@ -253,25 +248,24 @@ def rank_program(g, core, T, topo):
     for i in range(3):
         ts(r("MI", 256 * i, 256 * i + 256), r("ME", 0, 256), i, A.logical_shift_right, 1, A.bitwise_and)
     ts(r("MJ", 0, 768), r("MI", 0, 768), -1.0, A.mult, 1.0, A.add)
-    mset(r("TB", DUMP, DUMP + 256), 0.0)
+    for s in (1, 2):
+        act(r("X", W * s, W * s + W), r("X", 0, W), AF.Copy)
+    act(r("w", 0, K), r("C2", 0, K), AF.Copy)
     for i in range(2):
         mv("y", "r3", trow(rV + i, 0, W), r("VB", 256 * i, 256 * i + 256))
     rebuild("r5")
     for s in (0, 1):
         for i in range(2):
-            mv("s", "r6", trow(rV + i, W * s + W, W * s + 2 * W), trow(rV + i, 0, W))
+            mv("y", "r6", trow(rV + i, W * s + W, W * s + 2 * W), trow(rV + i, 0, W))
     for i in range(2):
         mv("y", "r4", trow(rFR + i, 0, W), r("FB", 256 * i, 256 * i + 256))
     for s in range(3):
         mv("y", "r7", trow(rJB, W * s, W * s + W), r("MJ", 256 * ((s + 1) % 3), 256 * ((s + 1) % 3) + 256))
     for s in (0, 1):
         for i in range(2):
-            mv("s", "r6", trow(rFR + i, W * s + W, W * s + 2 * W), trow(rFR + i, 0, W))
+            mv("y", "r6", trow(rFR + i, W * s + W, W * s + 2 * W), trow(rFR + i, 0, W))
     mv("y", "r8", trow(rJD, 0, 2 * W), trow(rJB, W, 3 * W))
     mv("y", "r8", trow(rJD, 2 * W, 3 * W), trow(rJB, 0, W))
-    for s in (1, 2):
-        act(r("X", W * s, W * s + W), r("X", 0, W), AF.Copy)
-    act(r("w", 0, K), r("C2", 0, K), AF.Copy)
 
     for i in range(3):
         ts(r("EQ3", 128 * i, 128 * i + 128), r("TY", 0, 128), float(i), A.is_equal)
@@ -280,9 +274,9 @@ def rank_program(g, core, T, topo):
         for i in range(3):
             e = (i - n) % 3
             tt(r("PR", 128 * i, 128 * i + 128), r("CF", 128 * i, 128 * i + 128), r("EQ3", 128 * e, 128 * e + 128), A.mult)
-        tt(r("PS", 0, 128), r("PR", 0, 128), r("PR", 128, 256), A.add)
-        tt(r("PS", 0, 128), r("PS", 0, 128), r("PR", 256, 384), A.add)
-        cp(r(L, 0, 128), r("PS", 0, 128))
+        tt(r("NE", 0, 128), r("PR", 0, 128), r("PR", 128, 256), A.add)
+        tt(r("NE", 0, 128), r("NE", 0, 128), r("PR", 256, 384), A.add)
+        cp(r(L, 0, 128), r("NE", 0, 128))
 
     ts(r("CO2", 0, 128), r("COL", 0, 128), 4, A.logical_shift_right)
     ts(r("CO2", 128, 256), r("COL", 0, 128), 15, A.bitwise_and)
@@ -292,16 +286,23 @@ def rank_program(g, core, T, topo):
     ts(r("RMX", 128, 256), cR, pR, A.is_equal)
     ts(r("BDm", 0, 128), cG, pG, A.is_equal)
     ts(r("IDn", 0, 128), cC, pP, A.is_equal)
-    ts(r("A1f", 0, 128), cQ, pC, A.is_equal)
-    cp(r("A1", 0, 128), r("A1f", 0, 128))
-    ts(r("A2f", 0, 128), cC, pP, A.is_ge)
-    tt(r("A2f", 0, 128), r("A2f", 0, 128), r("A1f", 0, 128), A.mult)
-    tt(r("A2", 0, 128), r("A2f", 0, 128), r("A1f", 0, 128), A.subtract)
+    ts(r("OK", 0, 128), cQ, pC, A.is_equal)
+    cp(r("A1", 0, 128), r("OK", 0, 128))
+    ts(r("JX", 0, 128), cC, pP, A.is_ge)
+    tt(r("JX", 0, 128), r("JX", 0, 128), r("OK", 0, 128), A.mult)
+    tt(r("A2", 0, 128), r("JX", 0, 128), r("OK", 0, 128), A.subtract)
     ts(r("A3", 0, 128), cQ, pC, A.is_gt)
     mset(r("ON", 0, 128), 1.0)
-    ts(r("PIf", 4, 5), pP, 64.0, A.is_ge, -1023.0, A.mult)
-    ts(r("J2", 0, 128), r("J2r", 0, 128), r("PIf", 4, 5), A.add)
-    ts(r("NJ", 0, 128), r("J2", 0, 128), -1.0, A.mult, -1.0, A.add)
+    ts(r("BX", 0, 128), cQ, pC, A.is_ge)
+    ts(r("OK", 0, 128), cC, 64.0, A.is_ge)
+    tt(r("EC0", 0, 128), r("BX", 0, 128), r("OK", 0, 128), A.max)
+    tt(r("EC1", 0, 128), r("BX", 0, 128), r("OK", 0, 128), A.mult)
+    cp(r("IOR", 0, 128), cC)
+    cp(r("BDb", 0, 128), r("BDm", 0, 128))
+    ts(r("GM16", 0, 8), r("GM", 0, 8), 16.0, A.mult)
+    mset(r("RKW", 128, 136), 9999.0)
+    mset(r("TG", 2048, 2064), 0.0)
+    mset(r("C2", 2048, 2064), 0.0)
     ts(r("RS", 0, 128), r("RSi", 0, 128), 0.0, A.is_gt)
     ts(r("KD", 0, 1), pP, -1.0, A.mult, 16384.0 - DUMP, A.add)
     ts(r("KD", 1, 2), pP, -1.0, A.mult, 16384.0 - DUMP - 128, A.add)
@@ -328,8 +329,8 @@ def rank_program(g, core, T, topo):
         cp(r("XW2", 8 * i, 8 * i + 8), r("GM", 0, 8))
     for i, c in enumerate((num(rV), ((rONE, 1), (rJB, -1)), (s4, (rDL, W)), ((rONE, 3 * W), (rS, -2 * W), (rDL, -W)), num(rFR))):
         wblock("WB", i, *c)
-    for i, c in enumerate((num(rNB), num(rV))):
-        pc = col(*(c + (s4, (rONE, -16384))))
+    for i, c in enumerate(((s4, (rDL, W)), (s4,))):
+        pc = col(*(num(rV) + c + ((rONE, -16384),)))
         sca(r("PG", 8 * i, 8 * i + 8), r("GM", 0, 8), pc)
         sca(r("PMX", 128 * i, 128 * i + 128), r("BDm", 0, 128), pc)
         for g_ in range(8):
@@ -345,19 +346,23 @@ def rank_program(g, core, T, topo):
     def zc(z):
         return r(z, 1, 129, 2)
 
-    def mklist(z, ps, pc, dst, h):
+    def turn(z, ps, pc):
         mm(r(ps, pc, pc + 64), r(z, 1, 129), r("IDn", 0, 64), True, False)
         mm(r(ps, pc, pc + 64), r(z, 0, 128), r("IDn", 64, 128), False, True)
+
+    def mklist(z, ps, pc, dst, h):
+        turn(z, ps, pc)
         return lambda: cp(r(dst, 64 * h, 64 * h + 64), r(ps, pc, pc + 64))
 
     TBw = r("TB", 0, DUMP + 256)
 
+    def ask(q, buf, L, h):
+        look(q, r(buf, 1024 * h, 1024 * h + 1024), TBw, r(L, 64 * h, 64 * h + 64))
+
     def refresh():
-        def ask(n, buf, L):
+        for n, (buf, L) in enumerate((("TG", "LA"), ("C2", "LB"))):
             for h in range(2):
-                look("vs"[(h + n) % 2], r(buf, 1024 * h, 1024 * h + 1024), TBw, r(L, 64 * h, 64 * h + 64))
-        ask(0, "TG", "LA")
-        ask(1, "C2", "LB")
+                ask("vs"[(h + n) % 2], buf, L, h)
         fin = []
         for h in range(2):
             units("tb%d" % h, "TG", 1024 * h, "WR", 2)
@@ -366,9 +371,12 @@ def rank_program(g, core, T, topo):
             units("cb%d" % h, "C2", 1024 * h, "WR", 1)
         for f in fin:
             f()
-        gath(0)
-        ask(2, "D2", "LD")
-        gath(1)
+        ask("s", "TG", "LA", 0)
+        match(0, False)
+        for h in range(2):
+            ask("vs"[h], "D2", "LD", h)
+        ask("s", "TG", "LA", 1)
+        match(1, False)
         for h in range(2):
             st, pd = "ST%d" % h, ("pa", "pb")[h]
             cp(r(st, 128, 192), r("cb%d" % h, 0, 64))
@@ -376,49 +384,71 @@ def rank_program(g, core, T, topo):
             ts(r(st, 0, 64), r(st, 128, 192), 4095, A.bitwise_and)
             cp(r(st, 64, 128), r(pd, 0, 64))
 
-    def gath(h):
+    def match(h, last):
         off = r("LA", 64 * h, 64 * h + 64)
         xw, cm, wv = r("X", 0, 3 * W), r("CM%d" % h, 0, 1024), r("w", 1024 * h, 1024 * h + 1024)
-        look("s", r("TG", 1024 * h, 1024 * h + 1024), TBw, off)
         op("v", lambda: V.tensor_tensor(ap(cm), ap(xw).indirect(ap(off)), ap(wv), A.is_ge), [xw, off, wv], [cm])
+        units("tb%d" % h, "TG", 1024 * h, "WL" if last else "WF", 8)
 
-    def update(h, last):
-        tb, cb, st, u, q, p, hm, z = ("%s%d" % (n, h) for n in ("tb", "cb", "ST", "u", "q", "p", "HM", "ZA"))
+    def names(h):
+        return ["%s%d" % (n, h) for n in ("tb", "cb", "ST", "u", "q", "p", "HM", "ZA")] + [("pa", "pb")[h]]
+
+    def before(h, last):
+        tb, cb, st, u, q, p, hm, z, dl = names(h)
         sl = lambda a, b: r(tb, 64 * a, 64 * b)
-        units(tb, "TG", 1024 * h, "WL" if last else "WF", 8)
-        units(cb, "CM%d" % h, 0, "XW2", 2)
         if last:
             ts(r(st, 0, 64), r(st, 128, 192), 12, A.logical_shift_right)
-        dl = ("pa", "pb")[h]
-        tt(r(u, 0, 128), r(st, 0, 128), sl(0, 2), A.subtract)
-        tt(r(dl, 0, 64), sl(6, 7), r(st, 64, 128), A.subtract)
-        tt(r(q, 0, 128), r(u, 0, 128), sl(2, 4), A.mult)
-        tt(sl(0, 2), r(q, 0, 128), sl(4, 6), A.add)
-        tt(r(dl, 64, 128), sl(1, 2), r(st, 128, 192), A.subtract)
-        act(r(hm, 0, 128), r(cb, 0, 128), AF.Sigmoid, -3400.0, 400.0)
-        tt(r(p, 0, 64), sl(0, 1), r(hm, 0, 64), A.mult)
-        tt(zc(z), r(p, 0, 64), sl(7, 8), A.add)
-        fin = mklist(z, "lb%d" % h, 0, "LA", h)
-        tt(r(dl, 0, 128), r(dl, 0, 128), r(hm, 0, 128), A.mult)
-        tt(r(st, 64, 192), r(st, 64, 192), r(dl, 0, 128), A.add)
-        if not last:
-            ts(r(st, 0, 64), r(st, 128, 192), 4095, A.bitwise_and)
-        fin()
+        return [lambda: tt(r(u, 0, 128), r(st, 0, 128), sl(0, 2), A.subtract),
+                lambda: tt(r(dl, 0, 64), sl(6, 7), r(st, 64, 128), A.subtract),
+                lambda: tt(r(q, 0, 128), r(u, 0, 128), sl(2, 4), A.mult),
+                lambda: tt(sl(0, 2), r(q, 0, 128), sl(4, 6), A.add),
+                lambda: tt(r(dl, 64, 128), sl(1, 2), r(st, 128, 192), A.subtract)]
+
+    def counts(h):
+        units("cb%d" % h, "CM%d" % h, 0, "XW2", 2)
+
+    def hit(h):
+        act(r("HM%d" % h, 0, 128), r("cb%d" % h, 0, 128), AF.Sigmoid, -3400.0, 400.0)
 
     def finds():
-        for q in range(FINDS):
-            for h in range(2):
-                update(h, q == FINDS - 1)
-                if q < FINDS - 1:
-                    gath(h)
+        counts(0)
+        hit(0)
+        for f in before(0, False):
+            f()
+        for n in range(2 * FINDS):
+            h, last = n % 2, n // 2 == FINDS - 1
+            tb, cb, st, u, q, p, hm, z, dl = names(h)
+            nxt = before(1 - h, (n + 1) // 2 == FINDS - 1) if n + 1 < 2 * FINDS else []
+            step = lambda k: nxt[k]() if nxt else None
+            tt(r(p, 0, 64), r(tb, 0, 64), r(hm, 0, 64), A.mult)
+            step(0)
+            tt(zc(z), r(p, 0, 64), r(tb, 448, 512), A.add)
+            fin = mklist(z, "lb%d" % h, 0, "LA", h)
+            tt(r(dl, 0, 128), r(dl, 0, 128), r(hm, 0, 128), A.mult)
+            if nxt:
+                counts(1 - h)
+            step(2)
+            tt(r(st, 64, 192), r(st, 64, 192), r(dl, 0, 128), A.add)
+            step(1)
+            fin()
+            if not last:
+                ask("s", "TG", "LA", h)
+            if nxt:
+                hit(1 - h)
+            step(3)
+            if not last:
+                ts(r(st, 0, 64), r(st, 128, 192), 4095, A.bitwise_and)
+            step(4)
+            if not last:
+                match(h, n // 2 + 1 == FINDS - 1)
 
     def boundary(t):
+        fast = t == ROUNDS - 1
         for h in range(2):
-            look("vs"[h], r("TG", 1024 * h, 1024 * h + 1024), TBw, r("LA", 64 * h, 64 * h + 64))
+            ask("vs"[h], "TG", "LA", h)
         for h in range(2):
             ts(r("CD%d" % h, 0, 128), r("ST%d" % h, 64, 192), 12, A.logical_shift_right)
             units("tb%d" % h, "TG", 1024 * h, "WB", 5)
-        mset(r("SW", 0, 128), 0.0)
         fin = []
         for h in range(2):
             tb, cd = "tb%d" % h, "CD%d" % h
@@ -429,27 +459,29 @@ def rank_program(g, core, T, topo):
         for f in fin:
             f()
         for h in range(2):
-            look("s", r("C2", 1024 * h, 1024 * h + 1024), TBw, r("LB", 64 * h, 64 * h + 64))
-        for i in range(2):
-            mv("y", "mg%d" % t, r("C2", 0, K, 1, rNB + i, 128, 16), r("TG", 0, K, 1, rV + i, 128, 16))
+            ask("s", "C2", "LB", h)
         op("v", lambda: V.tensor_tensor_scan(T.INC[:, :], T.RS[:, :], T.WT[:, :], 0.0, A.mult, A.add), [r("RS", 0, 128), r("WT", 0, 128)], [r("INC", 0, 128)])
         for h in range(2):
             c = 64 * h
-            mm(r("pa", c, c + 64), r("IDn", 0, 128), r("NJ", c, c + 64), True, False)
-            mm(r("pa", c, c + 64), r("A2", 0, 128), r("WT", c, c + 64), False, False)
+            mm(r("pa", c, c + 64), r("A2", 0, 128), r("WT", c, c + 64), True, False)
             mm(r("pa", c, c + 64), r("A1", 0, 128), r("INC", c, c + 64), False, False)
             for k in range(8):
                 if h:
                     mm(r("pa", c + k, c + 64, 8), r("ON", 0, 128), r("INC", 7, 64, 8), False, False)
                 mm(r("pa", c + k, c + 64, 8), r("A3", 0, 128), r("INC", c + 7, c + 64, 8), False, k == 7)
-        tt(r("XW", 0, 128), r("pa", 0, 128), r("WT", 0, 128), A.mult)
-        fin = []
         for h in range(2):
-            c = 64 * h
-            tt(zc("ZD%d" % h), r("XW", c, c + 64), r("J2", c, c + 64), A.add)
-            fin.append(mklist("ZD%d" % h, "cb%d" % h, 0, "LO", h))
-        for f in fin:
-            f()
+            mm(r("pa", 128, 136), r("EC%d" % h, 0, 128), r("INC", 64 * h + 7, 64 * h + 64, 8), h == 0, h == 1)
+        cp(r("CEN", 0, 8), r("pa", 128, 136))
+        for h in range(2):
+            cp(zc("ZD%d" % h), r("pa", 64 * h, 64 * h + 64))
+            turn("ZD%d" % h, "cb%d" % h, 0)
+        for g_ in range(8):
+            ts(r("CP", 128 * g_, 128 * g_ + 128), r("IOR", 0, 128), r("CEN", g_, g_ + 1), A.is_ge)
+            mm(r("pb", 16 * g_, 16 * g_ + 16), r("CP", 128 * g_, 128 * g_ + 128), r("ON", 0, 16), True, True)
+        for h in range(2):
+            cp(r("RKW", 64 * h, 64 * h + 64), r("cb%d" % h, 0, 64))
+        tt(r("BX", 0, 128), r("pb", 0, 128), r("RMX", 0, 128), A.mult)
+        mm(r("pb", 128, 136), r("BX", 0, 128), r("GM", 0, 8), True, True)
         fin = []
         for h in range(2):
             tb, cd = "tb%d" % h, "CD%d" % h
@@ -459,18 +491,29 @@ def rank_program(g, core, T, topo):
             fin.append(mklist("ZB%d" % h, "lb%d" % h, 64, "LD", h))
         for f in fin:
             f()
-        pull(t, 0, 2)
-        op("v", lambda: V.tensor_copy(T.SW[:, 0:4096].indirect(T.LO[:, 0:128]), T.C2[:, :]), [r("C2", 0, K), r("LO", 0, 128)], [r("SW", 0, 4096)])
-        SWs = r("SW", 0, 128)
+        cp(r("LQ", 0, 8), r("pb", 128, 136))
+        if fast:
+            pull(t, 0)
+        op("v", lambda: V.tensor_tensor(T.CP2[:, :], T.RKW[:, 0:136].indirect(T.LQ[:, 0:8]), ap(cC), A.is_le), [r("RKW", 0, 136), r("LQ", 0, 8), cC], [r("CP2", 0, 128)])
+        mm(r("pa", 0, 128), r("CP2", 0, 128), r("BDb", 0, 128), True, True)
+        if fast:
+            pull(t, 1)
+        tt(r("JX", 0, 128), r("pa", 0, 128), r("RMX", 0, 128), A.mult)
+        mm(r("pa", 128, 136), r("JX", 0, 128), r("GM", 0, 8), True, False)
+        mm(r("pa", 128, 136), r("BX", 0, 128), r("GM16", 0, 8), False, True)
+        cp(r("LJ", 0, 8), r("pa", 128, 136))
+        look("v", r("SM", 0, 128), r("TG", 0, 2064), r("LJ", 0, 8))
+        look("s", r("SC", 0, 128), r("C2", 0, 2064), r("LJ", 0, 8))
+        SWs = (r("SM", 0, 128), r("SC", 0, 128))
         for i in range(2):
-            mm(r("pb", 128 * i, 128 * i + 128), SWs, r("PMX", 128 * i, 128 * i + 128), True, True)
+            mm(r("pb", 128 * i, 128 * i + 128), SWs[i], r("PMX", 128 * i, 128 * i + 128), True, True)
         cp(r("OW", 0, 256), r("pb", 0, 256))
         banks = ("cb0", "cb1", "lb0", "lb1")
         order = (4, 6, 0, 1, 7, 2, 3, 5)
         for g_ in range(8):
             b, o = banks[g_ // 2], 256 * (g_ % 2)
             for i in range(2):
-                mm(r(b, o + 128 * i, o + 128 * i + 128), r("PB", 256 * g_ + 128 * i, 256 * g_ + 128 * i + 128), SWs, True, True)
+                mm(r(b, o + 128 * i, o + 128 * i + 128), r("PB", 256 * g_ + 128 * i, 256 * g_ + 128 * i + 128), SWs[i], True, True)
         for g_ in order:
             b, o = banks[g_ // 2], 256 * (g_ % 2)
             for i in range(2):
@@ -499,19 +542,24 @@ def rank_program(g, core, T, topo):
         ts(r("G5", 128, 256), r("G3", 0, 128), isn, A.mult)
         tt(r("G4", 0, 256), r("G4", 0, 256), r("G5", 0, 256), A.add)
         op("v", lambda: V.tensor_copy(ap(TBw).indirect(T.LP[:, 0:16]), T.G4[:, :]), [r("G4", 0, 256), r("LP", 0, 16)], [TBw])
-        if t < ROUNDS - 1:
-            rebuild("rb%d" % t)
-        else:
-            for i, d in ((0, "YL"), (1, "YH")):
+        if fast:
+            for i, d in ((0, "NL"), (1, "NH")):
                 mv("ys"[i], "yl", r(d, 0, 768), trow(i, 0, 3 * W))
-        pull(t, 2, 4)
+        else:
+            rebuild("rb%d" % t)
+        for c in (2, 3) if fast else range(4):
+            pull(t, c)
 
-    def pull(t, c0, c1):
+    def pull(t, c):
         xb = r("xb%d" % t, 0, W)
-        for c in range(c0, c1):
-            d, wv = r("D%d" % (c % 2), 0, 512), r("w", 512 * c, 512 * c + 512)
-            off, cl = r("LK", 32 * c, 32 * c + 32), r("DD%d" % c, 0, 512)
-            op("v", lambda: V.tensor_tensor(ap(d), ap(xb).indirect(ap(off)), ap(wv), A.subtract), [xb, off, wv], [d])
+        d, wv = r("D%d" % (c % 2), 0, 512), r("w", 512 * c, 512 * c + 512)
+        off, cl = r("LK", 32 * c, 32 * c + 32), r("DD%d" % c, 0, 512)
+        op("v", lambda: V.tensor_tensor(ap(d), ap(xb).indirect(ap(off)), ap(wv), A.subtract), [xb, off, wv], [d])
+        if t == ROUNDS - 1 and c > 1:
+            cl = r("tb%d" % (c % 2), 0, 512)
+            ts(cl, d, -8.0, A.max, 8.0, A.min)
+            tt(wv, wv, cl, A.add)
+        else:
             ts(cl, d, -8.0, A.max, 8.0, A.min)
             add("wa%d%d" % (t, c // 2), wv, cl)
 
@@ -521,20 +569,28 @@ def rank_program(g, core, T, topo):
         boundary(t)
         if t < ROUNDS - 1:
             refresh()
-    dma("y", "out1", T.yw[:, :], T.w[:, :], None, r("w", 0, K))
-    for i, L in enumerate(("LA", "LB", "LD")):
-        cp(r("CY", 128 * i, 128 * i + 128), r(L, 0, 128))
-    ts(r("TYY", 0, 384), r("CY", 0, 384), 12, A.logical_shift_right)
-    ts(r("CY", 0, 384), r("CY", 0, 384), 4095, A.bitwise_and)
-    for i in range(3):
-        ts(r("CE", 0, 384), r("TYY", 0, 384), float(i), A.is_equal)
-        tt(r("PR", 0, 384), r("CE", 0, 384), r("CY", 0, 384), A.mult)
-        tt(r("PS", 0, 128), r("PR", 0, 128), r("PR", 128, 256), A.add)
-        tt(r("YC", 128 * i, 128 * i + 128), r("PS", 0, 128), r("PR", 256, 384), A.add)
-    dma("y", "out2", T.yc[:, :], T.YC[:, :], None, r("YC", 0, 384))
-    ts(r("YG", 0, 768), r("YH", 0, 768), 64.0, A.mult)
-    tt(r("YF", 0, 768), r("YG", 0, 768), r("YL", 0, 768), A.add)
+    for i in range(2):
+        dma("y", "out%d" % i, T.yw[:, 1024 * i:1024 * i + 1024], T.w[:, 1024 * i:1024 * i + 1024], None, r("w", 1024 * i, 1024 * i + 1024))
+    for c0, c1, b in ((0, 512, "cb0"), (512, 768, "cb1")):
+        act(r(b, 0, c1 - c0), r("NH", c0, c1), AF.Copy, 0.0, 64.0)
+        tt(r("YF", c0, c1), r("NL", c0, c1), r(b, 0, c1 - c0), A.add)
     dma("y", "out3", T.yn[:, :], T.YF[:, :], None, r("YF", 0, 768))
+    a_, b_, d_ = (r("PR", 128 * i, 128 * i + 128) for i in range(3))
+    y0, y1, y2 = (r("CF", 128 * i, 128 * i + 128) for i in range(3))
+    for k, L in ((a_, "LA"), (b_, "LB"), (d_, "LD")):
+        cp(k, r(L, 0, 128))
+    lo, hi, sm = (r("EQ3", 128 * i, 128 * i + 128) for i in range(3))
+    tt(lo, a_, b_, A.min)
+    tt(hi, a_, b_, A.max)
+    tt(sm, a_, b_, A.add)
+    tt(y0, lo, d_, A.min)
+    tt(hi, hi, d_, A.max)
+    tt(sm, sm, d_, A.add)
+    tt(sm, sm, y0, A.subtract)
+    ts(y2, hi, -2.0 * W, A.add)
+    tt(sm, sm, hi, A.subtract)
+    ts(y1, sm, -1.0 * W, A.add)
+    dma("y", "out2", T.yc[:, :], T.CF[:, :], None, r("CF", 0, 384))
     for sem in SEMAPHORES:
         if sem == "xs":
             g.wait_ge(T.sem.xs, nloc)

from concourse.mybir import AluOpType as A, ActivationFunctionType as AF

ROUNDS, FINDS, W, K = 3, 6, 4096, 2048
DUMP = 3 * W
B, FL, IN, U16, SB = "bfloat16", "float32", "int32", "uint16", "sbuf"
rNA, rNB, rND, rV, rJB, rJD, rFR, rS, rDL, rONE = 0, 2, 4, 6, 8, 9, 10, 12, 13, 14

SCRATCH = {}
for _dt, _names in (
    (B, "X:12288 TB:12544 xb0:4096 xb1:4096 xb2:4096 TG:2064 C2:2064 D2:2048 CM0:1024 CM1:1024 SM:128 SC:128 CP:1024 CP2:128 IOR:128 BDb:128 EC0:128 EC1:128 "
        "NL:768 NH:768 MJ:768 FB:512 VB:512 HM0:128 HM1:128 WT:128 INC:128 A1:128 A2:128 A3:128 ON:128 WF:64 WL:64 WB:64 WR:64 XW2:16 PMX:256 PB:2048 EQ:4096 "
        "G3:256 G4:256 G5:256"),
    (FL, "w:2048 D0:512 D1:512 DD0:512 DD1:512 DD2:512 DD3:512 ya:256 yb:256 CF:384 EQ3:384 PR:384 u0:128 u1:128 p0:64 p1:64 q0:128 q1:128 "
         "ZA0:132 ZA1:132 ZB0:132 ZB1:132 ZC0:132 ZC1:132 ZD0:132 ZD1:132 NE:128 RKW:136 CEN:8 BX:128 JX:128 GM16:8 PIf:8 COF:512 GM:8 RM:16 RMX:256 BDm:128 IDn:128 "
         "RS:128 WC:64 PG:16 OW:256 OK:128 Y:256 YK:256 KD:2 DL:16 LPf:16 YF:768"),
    (IN, "NX:768 NI:768 ME:256 MI:768 FR:256 FI:512 VI:256 VJ:512 CU:384 TY:128 ST0:192 ST1:192 CD0:128 CD1:128 PIi:4 COL:128 CO2:384 RSi:128"),
    (U16, "LA:128 LB:128 LD:128 LK:128 LQ:8 LJ:8 LP:16"),
):
    for _n in _names.split():
        SCRATCH[_n.split(":")[0]] = (SB, [128, int(_n.split(":")[1])], _dt)
for _n in "tb0 tb1 cb0 cb1 lb0 lb1 pa pb".split():
    SCRATCH[_n] = ("psum", [128, 512], FL)
GROUPS = "ldx0 ldw ldn ldm ldf ldc r1 r2 r3 r4 r5 r6 r7 r8 wa00 wa01 wa10 wa11 wa20 rb0 rb1 out0 out1 out2 out3 yl".split()
SEMAPHORES = ["qv", "qs", "qt", "qg", "xs", "x0", "x1", "x2"] + GROUPS


def rank_program(g, core, T, topo):
    rank = T.rank_of(core)
    if rank is None:
        return
    Q = {"v": g.vector, "s": g.scalar, "t": g.tensor, "g": g, "y": g.sync}
    V, S, P = g.vector, g.scalar, g.tensor
    SEMOF = {"v": "qv", "s": "qs", "t": "qt", "g": "qg"}
    count, known, clock, acc, closed = {}, {q: {} for q in Q}, {}, {}, {}

    def r(name, c0, c1, step=1, p0=0, p1=128, ps=1):
        return (name, c0, c1, step, p0, p1, ps)

    def ap(k):
        if k[6] != 1:
            return T[k[0]][k[4]:k[5]:k[6], k[1]:k[2]]
        if k[3] != 1:
            return T[k[0]][k[4]:k[5], k[1]:k[2]:k[3]]
        return T[k[0]][k[4]:k[5], k[1]:k[2]]

    def psum(n):
        return SCRATCH[n][0] == "psum"

    def meet(a, b):
        if a[1] >= b[2] or b[1] >= a[2] or a[4] >= b[5] or b[4] >= a[5]:
            return False
        if a[6] == 16 and b[6] == 16 and a[4] % 16 != b[4] % 16:
            return False
        if a[3] == b[3] and a[3] > 1 and (a[1] - b[1]) % a[3]:
            return False
        return True

    def cover(a, b):
        return a[3] == 1 and a[6] == 1 and a[1] <= b[1] and a[2] >= b[2] and a[4] <= b[4] and a[5] >= b[5]

    def wait(q, ev):
        sem, n = ev
        if sem in GROUPS:
            n = count[sem]
            closed[sem] = True
        if known[q].get(sem, 0) >= n:
            return
        Q[q].wait_ge(T.sem[sem], n)
        known[q][sem] = n
        for k2, n2 in clock.get((sem, n), {}).items():
            if known[q].get(k2, 0) < n2:
                known[q][k2] = n2

    def deps(q, reads, writes):
        best = {}
        for isw, lst in ((False, reads), (True, writes)):
            for k in lst:
                for (k2, w2, ev, q2) in acc.get(k[0], []):
                    if psum(k[0]):
                        if q2 == q and (q == "t" or not (isw or w2) or not meet(k, k2)):
                            continue
                    elif not ((isw or w2) and meet(k, k2)):
                        continue
                    best[ev[0]] = max(best.get(ev[0], 0), ev[1])
        for s_ in sorted(best):
            wait(q, (s_, best[s_]))

    def note(q, reads, writes, ev, dma):
        tag = "dma" if dma else q
        for isw, lst in ((False, reads), (True, writes)):
            for k in lst:
                old = acc.get(k[0], [])
                if psum(k[0]):
                    old = [o for o in old if o[3] == tag and o[0] != k]
                    if isw and tag != "t":
                        old = [o for o in old if not cover(k, o[0])]
                elif isw:
                    old = [o for o in old if not cover(k, o[0])]
                elif not dma:
                    old = [o for o in old if not (o[3] == tag and not o[1] and o[0] == k)]
                acc[k[0]] = old + [(k, isw, ev, tag)]

    def op(q, fn, reads, writes):
        deps(q, reads, writes)
        sem = SEMOF[q]
        count[sem] = count.get(sem, 0) + 1
        ev = (sem, count[sem])
        fn().then_inc(T.sem[sem], 1)
        c = dict(known[q])
        c[sem] = count[sem]
        clock[ev] = c
        note(q, reads, writes, ev, False)

    def dma(q, grp, out, in_, outk=None, ink=None):
        assert not closed.get(grp)
        rd, wr = [ink] if ink else [], [outk] if outk else []
        deps(q, rd, wr)
        count[grp] = count.get(grp, 0) + 16
        Q[q].dma_start(out, in_).then_inc(T.sem[grp], 16)
        note(q, rd, wr, (grp, 0), True)

    def mv(q, grp, o, i):
        dma(q, grp, ap(o), ap(i), o, i)

    def add(grp, o, i):
        deps("g", [i], [o])
        count[grp] = count.get(grp, 0) + 16
        g.dma_start(ap(o), ap(i), accum_op=A.add).then_inc(T.sem[grp], 16)
        note("g", [i], [o], (grp, 0), True)

    def tt(o, a, b, f):
        op("v", lambda: V.tensor_tensor(ap(o), ap(a), ap(b), f), [a, b], [o])

    def ts(o, a, s1, f, s2=None, f2=None):
        rd = [a] + [k for k in (s1, s2) if isinstance(k, tuple)]
        x1 = ap(s1) if isinstance(s1, tuple) else s1
        x2 = ap(s2) if isinstance(s2, tuple) else s2
        if f2 is None:
            op("v", lambda: V.tensor_scalar(ap(o), ap(a), x1, None, f), rd, [o])
        else:
            op("v", lambda: V.tensor_scalar(ap(o), ap(a), x1, x2, f, f2), rd, [o])

    def cp(o, a):
        op("v", lambda: V.tensor_copy(ap(o), ap(a)), [a], [o])

    def mset(o, c):
        op("v", lambda: V.memset(ap(o), c), [], [o])

    def mm(o, l, h, start, stop):
        op("t", lambda: P.matmul(ap(o), ap(l), ap(h), start, stop), [l, h], [o])

    def act(o, a, f, bias=0.0, scale=1.0):
        b = ap(bias) if isinstance(bias, tuple) else bias
        op("s", lambda: S.activation(ap(o), ap(a), f, b, scale), [a] + ([bias] if isinstance(bias, tuple) else []), [o])

    def sca(o, a, c):
        op("s", lambda: S.activation(ap(o), ap(a), AF.Copy, 0.0, ap(c)), [a, c], [o])

    def look(q, o, win, off):
        if q == "v":
            op("v", lambda: V.tensor_copy(ap(o), ap(win).indirect(ap(off))), [win, off], [o])
        else:
            op("s", lambda: S.activation(ap(o), ap(win).indirect(ap(off)), AF.Copy), [win, off], [o])

    def iota(o, pat, base, cm):
        op("g", lambda: g.iota(ap(o), pat, base, cm), [], [o])

    dma("y", "ldn", T.NX[:, :], T.nxt[:, :], r("NX", 0, 768))
    dma("s", "ldx0", T.X[:, 0:W], T.x[:, :], r("X", 0, W))
    dma("y", "ldm", T.ME[:, :], T.mem[:, :], r("ME", 0, 256))
    dma("y", "ldf", T.FR[:, :], T.fro[:, :], r("FR", 0, 256))
    dma("y", "ldc", T.CU[:, :], T.cur[:, :], r("CU", 0, 384))
    dma("y", "ldc", T.TY[:, :], T.typ[:, :], r("TY", 0, 128))
    dma("s", "ldw", T.C2[:, 0:K], T.w0[:, :], r("C2", 0, K))
    iota(r("PIi", 0, 1), [[1, 1]], 0, 1)
    iota(r("COL", 0, 128), [[1, 128]], 0, 0)
    iota(r("VI", 0, 256), [[1, 256]], 0, 256)
    iota(r("RSi", 0, 128), [[0, 16], [1, 8]], 0, 0)

    wait("g", ("ldx0", 0))
    nloc = 0
    for t in range(ROUNDS):
        dst = T.cores[(rank - 1 - t) % len(T.cores)]
        rid, pid, _se = topo.addr(dst)
        g.remote_dma(T["xb%d" % t][:, :], T.X[:, 0:W], T.sem["x%d" % t], T.sem.xs, pid, rid, topo.mask(core, dst))
        nloc += len(topo.engines(core, dst))
        src = T.cores[(rank + 1 + t) % len(T.cores)]
        count["x%d" % t] = len(topo.engines(src, core))
        acc["xb%d" % t] = [(r("xb%d" % t, 0, W), True, ("x%d" % t, count["x%d" % t]), "dma")]

    ts(r("PIi", 1, 2), r("PIi", 0, 1), 4, A.logical_shift_right)
    ts(r("PIi", 2, 3), r("PIi", 0, 1), 15, A.bitwise_and)
    ts(r("PIi", 3, 4), r("PIi", 0, 1), 63, A.bitwise_and)
    cp(r("COF", 0, 128), r("COL", 0, 128))
    cp(r("PIf", 0, 4), r("PIi", 0, 4))
    pP, pG, pR, pC = (r("PIf", i, i + 1) for i in range(4))
    cC, cG, cR, cQ = (r("COF", 128 * i, 128 * i + 128) for i in range(4))
    ts(r("GM", 0, 8), r("COF", 0, 8), pG, A.is_equal)
    ts(r("RM", 0, 16), r("COF", 0, 16), pR, A.is_equal)
    cols = {}

    def col(*terms):
        key = ()
        for (rw, wt) in terms:
            prev = cols.get(key)
            key = key + ((rw, wt),)
            if key not in cols:
                n = len(cols)
                o = r("WC", n, n + 1)
                if prev is None:
                    ts(o, r("RM", rw, rw + 1), float(wt), A.mult)
                else:
                    ts(o, r("RM", rw, rw + 1), float(wt), A.mult, prev, A.add)
                cols[key] = o
        return cols[key]

    def num(a, f=1):
        return ((a, f), (a + 1, 64 * f))

    def trow(rw, c0, c1):
        return r("TB", c0, c1, 1, rw, 128, 16)

    def rebuild(grp):
        for i in range(2):
            for d0, d1, s0, a in ((0, 2 * W, W, 1), (2 * W, 3 * W, 0, 1), (0, W, 2 * W, 2), (W, 3 * W, 0, 2)):
                mv("y", grp, trow(2 * a + i, d0, d1), trow(i, s0, s0 + d1 - d0))

    mset(r("TB", 2 * W, 3 * W + 256), 0.0)
    for s in range(3):
        fc = col((rS, s), (rDL, 1 if s < 2 else -2), (rONE, 1))
        if s < 2:
            ts(r("TB", W * s, W * s + W), r("TB", 2 * W, 3 * W), fc, A.add)
        else:
            act(r("TB", W * s, W * s + W), r("TB", W * s, W * s + W), AF.Identity, fc)
    ts(r("NI", 0, 768), r("NX", 0, 768), 63, A.bitwise_and)
    cp(r("NL", 0, 768), r("NI", 0, 768))
    ts(r("VI", 0, 256), r("VI", 0, 256), 4095, A.bitwise_and)
    ts(r("NI", 0, 768), r("NX", 0, 768), 6, A.logical_shift_right)
    cp(r("NH", 0, 768), r("NI", 0, 768))
    mv("y", "r1", trow(rNA, 0, 3 * W), r("NL", 0, 768))
    mv("y", "r2", trow(rNA + 1, 0, 3 * W), r("NH", 0, 768))
    ts(r("VJ", 0, 256), r("VI", 0, 256), 63, A.bitwise_and)
    ts(r("VJ", 256, 512), r("VI", 0, 256), 6, A.logical_shift_right)
    cp(r("VB", 0, 512), r("VJ", 0, 512))
    ts(r("FI", 0, 256), r("FR", 0, 256), 63, A.bitwise_and)
    ts(r("FI", 256, 512), r("FR", 0, 256), 6, A.logical_shift_right)
    cp(r("FB", 0, 512), r("FI", 0, 512))
    for i in range(3):
        ts(r("MI", 256 * i, 256 * i + 256), r("ME", 0, 256), i, A.logical_shift_right, 1, A.bitwise_and)
    ts(r("MJ", 0, 768), r("MI", 0, 768), -1.0, A.mult, 1.0, A.add)
    for s in (1, 2):
        act(r("X", W * s, W * s + W), r("X", 0, W), AF.Copy)
    act(r("w", 0, K), r("C2", 0, K), AF.Copy)
    for i in range(2):
        mv("y", "r3", trow(rV + i, 0, W), r("VB", 256 * i, 256 * i + 256))
    rebuild("r5")
    for s in (0, 1):
        for i in range(2):
            mv("y", "r6", trow(rV + i, W * s + W, W * s + 2 * W), trow(rV + i, 0, W))
    for i in range(2):
        mv("y", "r4", trow(rFR + i, 0, W), r("FB", 256 * i, 256 * i + 256))
    for s in range(3):
        mv("y", "r7", trow(rJB, W * s, W * s + W), r("MJ", 256 * ((s + 1) % 3), 256 * ((s + 1) % 3) + 256))
    for s in (0, 1):
        for i in range(2):
            mv("y", "r6", trow(rFR + i, W * s + W, W * s + 2 * W), trow(rFR + i, 0, W))
    mv("y", "r8", trow(rJD, 0, 2 * W), trow(rJB, W, 3 * W))
    mv("y", "r8", trow(rJD, 2 * W, 3 * W), trow(rJB, 0, W))

    for i in range(3):
        ts(r("EQ3", 128 * i, 128 * i + 128), r("TY", 0, 128), float(i), A.is_equal)
        ts(r("CF", 128 * i, 128 * i + 128), r("CU", 128 * i, 128 * i + 128), float(W * i), A.add)
    for n, L in enumerate(("LA", "LB", "LD")):
        for i in range(3):
            e = (i - n) % 3
            tt(r("PR", 128 * i, 128 * i + 128), r("CF", 128 * i, 128 * i + 128), r("EQ3", 128 * e, 128 * e + 128), A.mult)
        tt(r("NE", 0, 128), r("PR", 0, 128), r("PR", 128, 256), A.add)
        tt(r("NE", 0, 128), r("NE", 0, 128), r("PR", 256, 384), A.add)
        cp(r(L, 0, 128), r("NE", 0, 128))

    ts(r("CO2", 0, 128), r("COL", 0, 128), 4, A.logical_shift_right)
    ts(r("CO2", 128, 256), r("COL", 0, 128), 15, A.bitwise_and)
    ts(r("CO2", 256, 384), r("COL", 0, 128), 63, A.bitwise_and)
    cp(r("COF", 128, 512), r("CO2", 0, 384))
    ts(r("RMX", 0, 128), cR, pR, A.is_equal)
    ts(r("RMX", 128, 256), cR, pR, A.is_equal)
    ts(r("BDm", 0, 128), cG, pG, A.is_equal)
    ts(r("IDn", 0, 128), cC, pP, A.is_equal)
    ts(r("OK", 0, 128), cQ, pC, A.is_equal)
    cp(r("A1", 0, 128), r("OK", 0, 128))
    ts(r("JX", 0, 128), cC, pP, A.is_ge)
    tt(r("JX", 0, 128), r("JX", 0, 128), r("OK", 0, 128), A.mult)
    tt(r("A2", 0, 128), r("JX", 0, 128), r("OK", 0, 128), A.subtract)
    ts(r("A3", 0, 128), cQ, pC, A.is_gt)
    mset(r("ON", 0, 128), 1.0)
    ts(r("BX", 0, 128), cQ, pC, A.is_ge)
    ts(r("OK", 0, 128), cC, 64.0, A.is_ge)
    tt(r("EC0", 0, 128), r("BX", 0, 128), r("OK", 0, 128), A.max)
    tt(r("EC1", 0, 128), r("BX", 0, 128), r("OK", 0, 128), A.mult)
    cp(r("IOR", 0, 128), cC)
    cp(r("BDb", 0, 128), r("BDm", 0, 128))
    ts(r("GM16", 0, 8), r("GM", 0, 8), 16.0, A.mult)
    mset(r("RKW", 128, 136), 9999.0)
    mset(r("TG", 2048, 2064), 0.0)
    mset(r("C2", 2048, 2064), 0.0)
    ts(r("RS", 0, 128), r("RSi", 0, 128), 0.0, A.is_gt)
    ts(r("KD", 0, 1), pP, -1.0, A.mult, 16384.0 - DUMP, A.add)
    ts(r("KD", 1, 2), pP, -1.0, A.mult, 16384.0 - DUMP - 128, A.add)
    ts(r("DL", 0, 16), r("COF", 0, 16), 16.0, A.mult, float(DUMP), A.add)
    ts(r("DL", 0, 16), r("DL", 0, 16), pR, A.add)
    for z in ("ZA0", "ZA1", "ZB0", "ZB1", "ZC0", "ZC1", "ZD0", "ZD1"):
        mset(r(z, 0, 132), 0.0)

    def wblock(buf, i, *terms):
        sca(r(buf, 8 * i, 8 * i + 8), r("GM", 0, 8), col(*terms))

    s4 = (rS, W)
    packA = num(rV, W) + num(rNA)
    packD = num(rV, W) + num(rND)
    nextA = (s4,) + num(rNA)
    for i, c in enumerate((packA, nextA)):
        wblock("WR", i, *c)
    minusA = ((rNA, -1), (rNA + 1, -64))
    for i, c in enumerate((num(rNB), packD, ((rJB, 1),), ((rJD, 1),), minusA + num(rNB) + ((rDL, W),), packD, packA, nextA)):
        wblock("WF", i, *c)
    for i, c in enumerate((num(rV), packD, ((rJB, 1),), ((rJD, 1),), ((rDL, W),), packD, packA, num(rV) + (s4,))):
        wblock("WL", i, *c)
    for i in range(2):
        cp(r("XW2", 8 * i, 8 * i + 8), r("GM", 0, 8))
    for i, c in enumerate((num(rV), ((rONE, 1), (rJB, -1)), (s4, (rDL, W)), ((rONE, 3 * W), (rS, -2 * W), (rDL, -W)), num(rFR))):
        wblock("WB", i, *c)
    for i, c in enumerate(((s4, (rDL, W)), (s4,))):
        pc = col(*(num(rV) + c + ((rONE, -16384),)))
        sca(r("PG", 8 * i, 8 * i + 8), r("GM", 0, 8), pc)
        sca(r("PMX", 128 * i, 128 * i + 128), r("BDm", 0, 128), pc)
        for g_ in range(8):
            sca(r("PB", 256 * g_ + 128 * i, 256 * g_ + 128 * i + 128), r("ON", 0, 128), r("PG", 8 * i + g_, 8 * i + g_ + 1))
    isn = col((rNA, 1), (rNA + 1, 1))
    ts(r("PIf", 5, 6), isn, -1.0, A.mult, 1.0, A.add)

    def units(ps, src, c0, wbuf, n):
        for b in range(16):
            k, e = b // 2, b % 2
            mm(r(ps, k, 64 * n, 8, 64 * e, 64 * e + 64), r(src, c0 + b, c0 + 1024, 16), r(wbuf, 0, 8 * n), True, True)

    def zc(z):
        return r(z, 1, 129, 2)

    def turn(z, ps, pc):
        mm(r(ps, pc, pc + 64), r(z, 1, 129), r("IDn", 0, 64), True, False)
        mm(r(ps, pc, pc + 64), r(z, 0, 128), r("IDn", 64, 128), False, True)

    def mklist(z, ps, pc, dst, h):
        turn(z, ps, pc)
        return lambda: cp(r(dst, 64 * h, 64 * h + 64), r(ps, pc, pc + 64))

    TBw = r("TB", 0, DUMP + 256)

    def ask(q, buf, L, h):
        look(q, r(buf, 1024 * h, 1024 * h + 1024), TBw, r(L, 64 * h, 64 * h + 64))

    def refresh():
        for n, (buf, L) in enumerate((("TG", "LA"), ("C2", "LB"))):
            for h in range(2):
                ask("vs"[(h + n) % 2], buf, L, h)
        fin = []
        for h in range(2):
            units("tb%d" % h, "TG", 1024 * h, "WR", 2)
            cp(zc("ZA%d" % h), r("tb%d" % h, 64, 128))
            fin.append(mklist("ZA%d" % h, "lb%d" % h, 0, "LA", h))
            units("cb%d" % h, "C2", 1024 * h, "WR", 1)
        for f in fin:
            f()
        ask("s", "TG", "LA", 0)
        match(0, False)
        for h in range(2):
            ask("vs"[h], "D2", "LD", h)
        ask("s", "TG", "LA", 1)
        match(1, False)
        for h in range(2):
            st, pd = "ST%d" % h, ("pa", "pb")[h]
            cp(r(st, 128, 192), r("cb%d" % h, 0, 64))
            units(pd, "D2", 1024 * h, "WR", 1)
            ts(r(st, 0, 64), r(st, 128, 192), 4095, A.bitwise_and)
            cp(r(st, 64, 128), r(pd, 0, 64))

    def match(h, last):
        off = r("LA", 64 * h, 64 * h + 64)
        xw, cm, wv = r("X", 0, 3 * W), r("CM%d" % h, 0, 1024), r("w", 1024 * h, 1024 * h + 1024)
        op("v", lambda: V.tensor_tensor(ap(cm), ap(xw).indirect(ap(off)), ap(wv), A.is_ge), [xw, off, wv], [cm])
        units("tb%d" % h, "TG", 1024 * h, "WL" if last else "WF", 8)

    def names(h):
        return ["%s%d" % (n, h) for n in ("tb", "cb", "ST", "u", "q", "p", "HM", "ZA")] + [("pa", "pb")[h]]

    def before(h, last):
        tb, cb, st, u, q, p, hm, z, dl = names(h)
        sl = lambda a, b: r(tb, 64 * a, 64 * b)
        if last:
            ts(r(st, 0, 64), r(st, 128, 192), 12, A.logical_shift_right)
        return [lambda: tt(r(u, 0, 128), r(st, 0, 128), sl(0, 2), A.subtract),
                lambda: tt(r(dl, 0, 64), sl(6, 7), r(st, 64, 128), A.subtract),
                lambda: tt(r(q, 0, 128), r(u, 0, 128), sl(2, 4), A.mult),
                lambda: tt(sl(0, 2), r(q, 0, 128), sl(4, 6), A.add),
                lambda: tt(r(dl, 64, 128), sl(1, 2), r(st, 128, 192), A.subtract)]

    def counts(h):
        units("cb%d" % h, "CM%d" % h, 0, "XW2", 2)

    def hit(h):
        act(r("HM%d" % h, 0, 128), r("cb%d" % h, 0, 128), AF.Sigmoid, -3400.0, 400.0)

    def finds():
        counts(0)
        hit(0)
        for f in before(0, False):
            f()
        for n in range(2 * FINDS):
            h, last = n % 2, n // 2 == FINDS - 1
            tb, cb, st, u, q, p, hm, z, dl = names(h)
            nxt = before(1 - h, (n + 1) // 2 == FINDS - 1) if n + 1 < 2 * FINDS else []
            step = lambda k: nxt[k]() if nxt else None
            tt(r(p, 0, 64), r(tb, 0, 64), r(hm, 0, 64), A.mult)
            step(0)
            tt(zc(z), r(p, 0, 64), r(tb, 448, 512), A.add)
            fin = mklist(z, "lb%d" % h, 0, "LA", h)
            tt(r(dl, 0, 128), r(dl, 0, 128), r(hm, 0, 128), A.mult)
            if nxt:
                counts(1 - h)
            step(2)
            tt(r(st, 64, 192), r(st, 64, 192), r(dl, 0, 128), A.add)
            step(1)
            fin()
            if not last:
                ask("s", "TG", "LA", h)
            if nxt:
                hit(1 - h)
            step(3)
            if not last:
                ts(r(st, 0, 64), r(st, 128, 192), 4095, A.bitwise_and)
            step(4)
            if not last:
                match(h, n // 2 + 1 == FINDS - 1)

    def boundary(t):
        fast = t == ROUNDS - 1
        for h in range(2):
            ask("vs"[h], "TG", "LA", h)
        for h in range(2):
            ts(r("CD%d" % h, 0, 128), r("ST%d" % h, 64, 192), 12, A.logical_shift_right)
            units("tb%d" % h, "TG", 1024 * h, "WB", 5)
        fin = []
        for h in range(2):
            tb, cd = "tb%d" % h, "CD%d" % h
            tt(zc("ZA%d" % h), r(tb, 128, 192), r(cd, 64, 128), A.add)
            fin.append(mklist("ZA%d" % h, "lb%d" % h, 0, "LB", h))
            tt(r("NE", 64 * h, 64 * h + 64), r(tb, 0, 64), r(cd, 64, 128), A.not_equal)
            tt(r("WT", 64 * h, 64 * h + 64), r(tb, 64, 128), r("NE", 64 * h, 64 * h + 64), A.mult)
        for f in fin:
            f()
        for h in range(2):
            ask("s", "C2", "LB", h)
        op("v", lambda: V.tensor_tensor_scan(T.INC[:, :], T.RS[:, :], T.WT[:, :], 0.0, A.mult, A.add), [r("RS", 0, 128), r("WT", 0, 128)], [r("INC", 0, 128)])
        for h in range(2):
            c = 64 * h
            mm(r("pa", c, c + 64), r("A2", 0, 128), r("WT", c, c + 64), True, False)
            mm(r("pa", c, c + 64), r("A1", 0, 128), r("INC", c, c + 64), False, False)
            for k in range(8):
                if h:
                    mm(r("pa", c + k, c + 64, 8), r("ON", 0, 128), r("INC", 7, 64, 8), False, False)
                mm(r("pa", c + k, c + 64, 8), r("A3", 0, 128), r("INC", c + 7, c + 64, 8), False, k == 7)
        for h in range(2):
            mm(r("pa", 128, 136), r("EC%d" % h, 0, 128), r("INC", 64 * h + 7, 64 * h + 64, 8), h == 0, h == 1)
        cp(r("CEN", 0, 8), r("pa", 128, 136))
        for h in range(2):
            cp(zc("ZD%d" % h), r("pa", 64 * h, 64 * h + 64))
            turn("ZD%d" % h, "cb%d" % h, 0)
        for g_ in range(8):
            ts(r("CP", 128 * g_, 128 * g_ + 128), r("IOR", 0, 128), r("CEN", g_, g_ + 1), A.is_ge)
            mm(r("pb", 16 * g_, 16 * g_ + 16), r("CP", 128 * g_, 128 * g_ + 128), r("ON", 0, 16), True, True)
        for h in range(2):
            cp(r("RKW", 64 * h, 64 * h + 64), r("cb%d" % h, 0, 64))
        tt(r("BX", 0, 128), r("pb", 0, 128), r("RMX", 0, 128), A.mult)
        mm(r("pb", 128, 136), r("BX", 0, 128), r("GM", 0, 8), True, True)
        fin = []
        for h in range(2):
            tb, cd = "tb%d" % h, "CD%d" % h
            cp(zc("ZC%d" % h), r(tb, 256, 320))
            fin.append(mklist("ZC%d" % h, "lb%d" % h, 0, "LK", h))
            tt(zc("ZB%d" % h), r(tb, 192, 256), r(cd, 0, 64), A.add)
            fin.append(mklist("ZB%d" % h, "lb%d" % h, 64, "LD", h))
        for f in fin:
            f()
        cp(r("LQ", 0, 8), r("pb", 128, 136))
        if fast:
            pull(t, 0)
        op("v", lambda: V.tensor_tensor(T.CP2[:, :], T.RKW[:, 0:136].indirect(T.LQ[:, 0:8]), ap(cC), A.is_le), [r("RKW", 0, 136), r("LQ", 0, 8), cC], [r("CP2", 0, 128)])
        mm(r("pa", 0, 128), r("CP2", 0, 128), r("BDb", 0, 128), True, True)
        if fast:
            pull(t, 1)
        tt(r("JX", 0, 128), r("pa", 0, 128), r("RMX", 0, 128), A.mult)
        mm(r("pa", 128, 136), r("JX", 0, 128), r("GM", 0, 8), True, False)
        mm(r("pa", 128, 136), r("BX", 0, 128), r("GM16", 0, 8), False, True)
        cp(r("LJ", 0, 8), r("pa", 128, 136))
        look("v", r("SM", 0, 128), r("TG", 0, 2064), r("LJ", 0, 8))
        look("s", r("SC", 0, 128), r("C2", 0, 2064), r("LJ", 0, 8))
        SWs = (r("SM", 0, 128), r("SC", 0, 128))
        for i in range(2):
            mm(r("pb", 128 * i, 128 * i + 128), SWs[i], r("PMX", 128 * i, 128 * i + 128), True, True)
        cp(r("OW", 0, 256), r("pb", 0, 256))
        banks = ("cb0", "cb1", "lb0", "lb1")
        order = (4, 6, 0, 1, 7, 2, 3, 5)
        for g_ in range(8):
            b, o = banks[g_ // 2], 256 * (g_ % 2)
            for i in range(2):
                mm(r(b, o + 128 * i, o + 128 * i + 128), r("PB", 256 * g_ + 128 * i, 256 * g_ + 128 * i + 128), SWs[i], True, True)
        for g_ in order:
            b, o = banks[g_ // 2], 256 * (g_ % 2)
            for i in range(2):
                e, own = r("EQ", 512 * g_ + 256 * i, 512 * g_ + 256 * i + 256), r("OW", 128 * i + 16 * g_, 128 * i + 16 * g_ + 1)
                if g_ < 5:
                    ts(e, r(b, o, o + 256), own, A.is_equal)
                else:
                    y = r(("ya", "yb")[i], 0, 256)
                    act(y, r(b, o, o + 256), AF.Abs, own, -1.0)
                    act(e, y, AF.Relu, 1.0, -1.0)
        for g_ in order:
            for i in range(4):
                mm(r("pa", 16 * g_, 16 * g_ + 16), r("EQ", 512 * g_ + 128 * i, 512 * g_ + 128 * i + 128), r("ON", 0, 16), i == 0, i == 3)
        for i in range(2):
            ts(r("Y", 128 * i, 128 * i + 128), r("OW", 128 * i, 128 * i + 128), r("KD", i, i + 1), A.add)
        tt(r("Y", 0, 256), r("Y", 0, 256), r("RMX", 0, 256), A.mult)
        ts(r("OK", 0, 128), r("pa", 0, 128), 2.5, A.is_le)
        for i in range(2):
            tt(r("YK", 128 * i, 128 * i + 128), r("Y", 128 * i, 128 * i + 128), r("OK", 0, 128), A.mult)
            mm(r("pb", 8 * i, 8 * i + 8), r("YK", 128 * i, 128 * i + 128), r("GM", 0, 8), True, True)
        tt(r("LPf", 0, 16), r("pb", 0, 16), r("DL", 0, 16), A.add)
        cp(r("LP", 0, 16), r("LPf", 0, 16))
        look("v", r("G3", 0, 256), TBw, r("LP", 0, 16))
        ts(r("G4", 0, 256), r("G3", 0, 256), r("PIf", 5, 6), A.mult)
        ts(r("G5", 0, 128), r("G3", 128, 256), isn, A.mult)
        ts(r("G5", 128, 256), r("G3", 0, 128), isn, A.mult)
        tt(r("G4", 0, 256), r("G4", 0, 256), r("G5", 0, 256), A.add)
        op("v", lambda: V.tensor_copy(ap(TBw).indirect(T.LP[:, 0:16]), T.G4[:, :]), [r("G4", 0, 256), r("LP", 0, 16)], [TBw])
        if fast:
            for i, d in ((0, "NL"), (1, "NH")):
                mv("ys"[i], "yl", r(d, 0, 768), trow(i, 0, 3 * W))
        else:
            rebuild("rb%d" % t)
        for c in (2, 3) if fast else range(4):
            pull(t, c)

    def pull(t, c):
        xb = r("xb%d" % t, 0, W)
        d, wv = r("D%d" % (c % 2), 0, 512), r("w", 512 * c, 512 * c + 512)
        off, cl = r("LK", 32 * c, 32 * c + 32), r("DD%d" % c, 0, 512)
        op("v", lambda: V.tensor_tensor(ap(d), ap(xb).indirect(ap(off)), ap(wv), A.subtract), [xb, off, wv], [d])
        if t == ROUNDS - 1 and c > 1:
            cl = r("tb%d" % (c % 2), 0, 512)
            ts(cl, d, -8.0, A.max, 8.0, A.min)
            tt(wv, wv, cl, A.add)
        else:
            ts(cl, d, -8.0, A.max, 8.0, A.min)
            add("wa%d%d" % (t, c // 2), wv, cl)

    refresh()
    for t in range(ROUNDS):
        finds()
        boundary(t)
        if t < ROUNDS - 1:
            refresh()
    for i in range(2):
        dma("y", "out%d" % i, T.yw[:, 1024 * i:1024 * i + 1024], T.w[:, 1024 * i:1024 * i + 1024], None, r("w", 1024 * i, 1024 * i + 1024))
    for c0, c1, b in ((0, 512, "cb0"), (512, 768, "cb1")):
        act(r(b, 0, c1 - c0), r("NH", c0, c1), AF.Copy, 0.0, 64.0)
        tt(r("YF", c0, c1), r("NL", c0, c1), r(b, 0, c1 - c0), A.add)
    dma("y", "out3", T.yn[:, :], T.YF[:, :], None, r("YF", 0, 768))
    a_, b_, d_ = (r("PR", 128 * i, 128 * i + 128) for i in range(3))
    y0, y1, y2 = (r("CF", 128 * i, 128 * i + 128) for i in range(3))
    for k, L in ((a_, "LA"), (b_, "LB"), (d_, "LD")):
        cp(k, r(L, 0, 128))
    lo, hi, sm = (r("EQ3", 128 * i, 128 * i + 128) for i in range(3))
    tt(lo, a_, b_, A.min)
    tt(hi, a_, b_, A.max)
    tt(sm, a_, b_, A.add)
    tt(y0, lo, d_, A.min)
    tt(hi, hi, d_, A.max)
    tt(sm, sm, d_, A.add)
    tt(sm, sm, y0, A.subtract)
    ts(y2, hi, -2.0 * W, A.add)
    tt(sm, sm, hi, A.subtract)
    ts(y1, sm, -1.0 * W, A.add)
    dma("y", "out2", T.yc[:, :], T.CF[:, :], None, r("CF", 0, 384))
    for sem in SEMAPHORES:
        if sem == "xs":
            g.wait_ge(T.sem.xs, nloc)
        elif count.get(sem, 0):
            known["g"].pop(sem, None)
            wait("g", (sem, count[sem]))
